import numpy as np, ml_dtypes
CORES = [40,41,42,43,44,45,46,47]
N = 8
BF = ml_dtypes.bfloat16
def gentries(a):
    return np.ascontiguousarray(a.reshape(8, 16, -1).transpose(0, 2, 1)).reshape(8, -1)
def gtable(e):
    e = np.asarray(e); return np.ascontiguousarray(e.reshape(8, -1, 16).transpose(0, 2, 1)).reshape(128, -1).astype(np.int32)
V, C, L, R = 2048, 6144, 256, 3
F, MX, TOP = 16 * N, 31248 * N, 2 ** 22 - 1
def parents(rng):
    p = np.zeros((8, V), np.int64); o = rng.permutation(8)
    for g in range(8):
        m = (V >> 4, V >> 3, V >> 2, V >> 1)[int(o[g]) % 4]; pool = rng.permutation(V)[:m]
        p[g] = pool[rng.integers(0, m, V)]; p[g, pool[0]] = pool[0]
    return p
def parts(rng):
    x = rng.integers(-31, 32, (8, F, V)); k = rng.integers(-63, 64, (8, F, C))
    b = np.where(rng.random((8, C)) < 0.2, rng.integers(-MX, MX + 1, (8, C)), rng.integers(-4096, 4097, (8, C)))
    w = np.where(rng.random((8, C)) < 0.25, 1000 * rng.integers(0, 4, (8, C)), rng.integers(0, TOP + 1, (8, C)))
    d = rng.integers(0, C, (8, 16, V)); one = rng.random((8, 1, V)) < 0.15
    return x, k, b, w, np.where(one, d[:, :1], d), parents(rng)
def pack(x, k, b, w, d, p):
    def deal(a): return np.ascontiguousarray(a.reshape(8, N, 16, -1).transpose(1, 0, 2, 3)).reshape(N, 128, -1).astype(np.float32).astype(BF)
    def same(a): return np.stack([np.ascontiguousarray(a).astype(np.int32)] * N)
    return {"xv": deal(x), "kc": deal(k), "bt": same(b), "co": same(w), "cd": same(d.reshape(128, V)), "pa": same(gtable(p))}
def sides(x, k, b, g, c, plus, minus):
    k[g, 0, c] = 63; b[g, c] = 0
    for s, v in ((1, plus), (-1, minus)):
        a = x[g][:, v]; r = np.add.reduce(k[g, 1:, c][:, None] * a[1:], axis=0)
        a = np.where(r * s < 0, -a, a); a[0] = s * np.maximum(np.abs(a[0]), 1); x[g][:, v] = a
def setup_inputs(rng):
    return pack(*parts(rng))
def setup_inputs_corners(rng):
    x, k, b, w, d, p = parts(rng); v = np.arange(V)
    b[:, 0] = MX; b[:, C - 1] = -MX; w[:, 0] = 0; w[:, C - 1] = 0
    u = rng.integers(0, 5, (8, 1, V)); dead = (C - 1) * rng.integers(0, 2, (8, 16, V)); n = np.arange(16)[None, :, None]
    d = np.where(((u == 0) & (n < 15)) | ((u == 1) & (n > 0)) | ((u == 2) & (n >= 0)), dead, d)
    d[:, :, 0] = rng.integers(1, C - 1, (8, 16)); d[:, :, V - 1] = rng.integers(1, C - 1, (8, 16))
    t = L * np.arange(R); edge = np.unique(np.maximum(np.concatenate([t - 1, t, t + L - 1, t + L]), 0))
    shapes = [np.where(rng.random(V) < 0.5, v, p[0]), (v + L) % V, np.maximum(v - 1, 0), np.full(V, V - 1), np.where(v == V - 1, v, 0), edge[rng.integers(0, len(edge), V)], V - 1 - v, (v + 1) % V]
    o = rng.permutation(8); cut = rng.integers(1, C - 1, 8)
    for g, a in zip(o, shapes): p[g] = a
    g, c = int(o[0]), int(cut[0]); m = np.arange(16); i = L * (R - 2) + m; s = V - 17 + m; e = R * L + m
    p[g] = np.where(np.isin(p[g], np.concatenate([i, s, e])), V - 1, p[g])
    p[g, L * (R - 1):L * R] = v[L * (R - 1):L * R]; p[g, i] = s; p[g, s] = e
    sides(x, k, b, g, c, np.concatenate([i, e]), s); d[g, 0, s] = c; w[g, c] = 0
    g, c = int(o[3]), int(cut[3]); sides(x, k, b, g, c, v[:V - 1], v[V - 1:]); d[g, 0, V - 1] = c; w[g, c] = 0
    g, c = int(o[6]), int(cut[6]); i = np.arange(R * L); sides(x, k, b, g, c, i, V - 1 - i); d[g, rng.integers(0, 16, R * L), V - 1 - i] = c
    for r in range(1, R, 2):
        q = L * r + int(rng.integers(0, L)); p[g, q] = q
    g, c = int(o[7]), int(cut[7]); q = L * np.arange(1, R); sides(x, k, b, g, c, np.concatenate([q - 1, q + 1]), q)
    d[g, 0, q] = c; d[g, 0, q - 1] = c; d[g, :, q - 2] = 0; w[g, c] = 0
    return pack(x, k, b, w, d, p)
def setup_inputs_crowd(rng):
    x, k, b, w, d, p = parts(rng); o = rng.permutation(8)
    for n in range(8):
        g = int(o[n]); big = V - 1 - n
        p[g, :R * L] = big; rest = rng.random(V - R * L) < 0.5; p[g, R * L:] = np.where(rest, big, p[g, R * L:])
        if n % 4 == 2: p[g, 1:R * L:2] = V - 10
        if n % 2 == 1:
            for t in range(R): p[g, L * t + (0, L - 1, int(rng.integers(1, L - 1)))[(n // 2 + t) % 3]] = V - 20 - t
        if n < 2: b[g, 0] = MX; d[g, :, big] = 0
        elif n < 4: d[g, :, big] = d[g, 0, big]
    return pack(x, k, b, w, d, p)
def setup_inputs_ends(rng):
    x, k, b, w, d, p = parts(rng); h = 2 * rng.integers(0, 2, (8, F, 1)) - 1; h0 = h[:, :, 0]
    def signs(n):
        u = rng.integers(0, 3, (8, 1, n)); z = 2 * rng.integers(0, 2, (8, F, n)) - 1
        return np.where(u == 0, h, np.where(u == 1, -h, z))
    a, q = signs(V), signs(C); q[:, :, C - 1] = h0; q[:, :, 0] = -h0
    q[:, :, [C - 3, C - 2]] = h; q[:, :, [1, 2]] = -h
    a[:, :, V - 1] = h0 * (1 - 2 * (np.arange(8)[:, None] & 1)); a[:, :, 0] = -a[:, :, V - 1]
    b = np.where(rng.random((8, C)) < 0.7, MX * (2 * rng.integers(0, 2, (8, C)) - 1), rng.integers(-6000, 6001, (8, C))); b[:, 0] = -MX; b[:, C - 1] = -MX
    b[:, 1] = -MX; b[:, 2] = 1 - MX; b[:, C - 3] = MX - 32; b[:, C - 2] = MX - 1
    share = np.where(np.arange(8) % 2 == 1, 0.92, 0.5)[:, None]; w = np.where(rng.random((8, C)) < share, TOP, 0)
    w = np.where(rng.random((8, C)) < 0.15, np.abs(w - rng.integers(0, 4, (8, C))), w); w[1::2, 0] = TOP; w[::2, 0] = 0; w[:, C - 1] = TOP
    d = np.where(rng.random(d.shape) < 0.7, (C - 1) * rng.integers(0, 2, d.shape), d)
    p = np.where(rng.random(p.shape) < 0.68, (V - 1) * rng.integers(0, 2, p.shape), p)
    p = np.where((p >= V - 1 - 4 * R) & (p < V - 1), V - 1, p)
    for t in range(R):
        i, s = L * t + L - 1, V - 2 - t; p[:, i] = s; a[:, :, i] = h0; a[:, :, s] = -h0
    x = 31 * a
    for t in range(R):
        for n, c in enumerate(([C - 2], [1, 2], [1, 2, C - 3, C - 2])):
            i, s, f = L * t + L - 2 - n, V - 2 - R - 3 * t - n, int(rng.integers(0, F)); p[:, i] = s
            x[:, :, i] = 31 * h0; x[:, f, i] = 30 * h0[:, f]; x[:, :, s] = 31 * h0
            d[:, :, s] = np.array(c)[rng.integers(0, len(c), (8, 16))]
    return pack(x, 63 * q, b, w, d, p)
def setup_inputs_spread(rng):
    x, k, b, w, d, p = parts(rng)
    x = np.rint(x * np.exp2(-rng.integers(0, 5, (8, 1, V)).astype(np.float64))) * (rng.random((8, 1, V)) > 0.0625)
    k = np.rint(k * np.exp2(-rng.integers(0, 6, (8, 1, C)).astype(np.float64)))
    b = np.clip((np.exp2(17 * rng.random((8, C)))).astype(np.int64) * (2 * rng.integers(0, 2, (8, C)) - 1), -MX, MX)
    w = np.exp2(22 * rng.random((8, C))).astype(np.int64) - 1
    d = np.minimum((C * rng.random(d.shape) ** 2).astype(np.int64), C - 1)
    for g in range(8): p[g] = rng.permutation(V)[np.minimum((V * rng.random(V) ** 3).astype(np.int64), V - 1)]
    return pack(x, k, b, w, d, p)
def setup_inputs_ties(rng):
    x, k, b, w, d, p = parts(rng); i = np.arange(R * L)
    x[::2] = rng.integers(-1, 2, (4, F, V)); k[::2] = rng.integers(-1, 2, (4, F, C)); b[::2] = rng.integers(-3, 4, (4, C))
    w = np.array([0, 1, TOP - 1, TOP])[rng.integers(0, 4, (8, C))]; w[1::4] = TOP - rng.integers(0, 2, (2, C)); w[2::4] = TOP - rng.integers(0, 2, (2, C))
    for g in (1, 3, 5, 7):
        s = p[g, i]; c = d[g][:, s]; own = np.where(rng.random(c.shape) < 0.5, i[None, :], s[None, :])
        z = np.einsum("fkl,fkl->kl", k[g][:, c], x[g][:, own])
        b[g, c] = np.clip(z + rng.integers(-1, 2, c.shape), -MX, MX)
    return pack(x, k, b, w, d, p)
def check_inputs(d):
    bad = []
    for k, lo, hi in (("xv", -31, 31), ("kc", -63, 63), ("bt", -MX, MX), ("co", 0, TOP), ("cd", 0, C - 1), ("pa", 0, V - 1)):
        a = np.asarray(d[k]).astype(np.float64)
        if not (np.min(a) >= lo and np.max(a) <= hi): bad.append("range of " + k)
        if k in ("xv", "kc") and not np.all(a == np.floor(a)): bad.append("whole numbers in " + k)
        if k not in ("xv", "kc") and not np.all(a == a[:1]): bad.append(k + " alike on all ranks")
    return bad
def reference(xv, kc, bt, co, cd, pa):
    x = np.ascontiguousarray(xv.astype(np.float32).reshape(N, 8, 16, V).transpose(1, 0, 2, 3)).reshape(8, F, V)
    k = np.ascontiguousarray(kc.astype(np.float32).reshape(N, 8, 16, C).transpose(1, 0, 2, 3)).reshape(8, F, C)
    b = bt[0].astype(np.int64); w = co[0].astype(np.int64); d = cd[0].astype(np.int64).reshape(8, 16, V); p = gentries(pa[0]).astype(np.int64)
    yc = np.full((8, R * L), -1, np.int64)
    for rnd in range(R):
        lane = np.arange(L * rnd, L * rnd + L); new = np.array(p)
        for g in range(8):
            s = p[g, lane]; c = d[g][:, s]; kp = k[g][:, c]
            si = np.einsum("fkl,fl->kl", kp, x[g][:, lane]) > b[g][c]; ss = np.einsum("fkl,fl->kl", kp, x[g][:, s]) > b[g][c]
            apart = si != ss
            first = np.zeros(L, bool); first[np.unique(s, return_index=True)[1]] = True
            act = first & ((s < lane[0]) | (s > lane[-1])) & np.any(apart, axis=0)
            best = np.argmin(np.where(apart, w[g][c], 2 ** 24), axis=0)
            a = np.nonzero(act)[0]; i = lane[a]; sa = s[a]; ca = c[best[a], a]; side = si[best[a], a]
            yc[g, i] = w[g][ca]
            who = np.full(V, -1, np.int64); who[sa] = np.arange(len(a))
            u = who[p[g]]; j = np.nonzero(u >= 0)[0]; u = u[j]; cj = ca[u]
            sj = np.einsum("fj,fj->j", k[g][:, cj], x[g][:, j]) > b[g][cj]
            m = (sj == side[u]) & (j != i[u]); new[g, j[m]] = i[u[m]]
            up = p[g, sa]; o = (np.einsum("fj,fj->j", k[g][:, ca], x[g][:, up]) > b[g][ca]) == side
            new[g, i[o]] = up[o]; new[g, sa[o]] = i[o]
        p = new
    return {"yp": np.stack([gtable(p)] * N).astype(np.float32), "yc": np.stack([gtable(yc)] * N).astype(np.float32)}

@@ -1,0 +1,556 @@
+from concourse.bass import DstId, RemoteDMATransfer
+from concourse.mybir import AluOpType as OP, AxisListType, ActivationFunctionType as AF
+
+N, V, C, L, R = 8, 2048, 6144, 256, 3
+W = V + L
+BIAS = 32768.0
+Q = C // 16
+MERGE = True
+
+SCRATCH = {}
+
+
+def _sb(name, cols, dtype):
+    SCRATCH[name] = ("sbuf", [128, cols], dtype)
+
+
+for _n, _c, _d in [
+    ("K", C, "bfloat16"), ("X", V, "bfloat16"), ("CD", V, "int32"), ("PA", 128, "int32"), ("META", C, "bfloat16"),
+    ("BC", 2 * Q, "int32"), ("BR", 2 * Q, "float32"), ("CP", 8 * Q, "bfloat16"),
+    ("W1", W, "bfloat16"), ("UB", W, "bfloat16"), ("KG", 4096, "bfloat16"), ("PI", 4096, "float16"), ("PS", 4096, "float16"),
+    ("XE0", 4096, "bfloat16"), ("XE1", 4096, "bfloat16"), ("XE2", 4096, "bfloat16"), ("BA", 2048, "float16"),
+    ("PC", V, "float16"), ("PU", L, "float16"), ("XS", L, "bfloat16"), ("KC", 272, "bfloat16"), ("KA", 1536, "bfloat16"),
+    ("MB", 528, "bfloat16"), ("SB", 528, "bfloat16"), ("MG", 512, "bfloat16"), ("E", L, "uint16"), ("EO", 32, "uint16"),
+    ("i1", 144, "float32"), ("i3", 256, "float32"), ("i4", 256, "float32"), ("i5", 256, "float32"),
+    ("ii", 32, "int32"), ("col", 32, "float32"), ("I16", 16, "float32"),
+    ("ZA", 144, "float16"), ("ZT", 144, "bfloat16"), ("ZW", 144, "bfloat16"), ("ZC", 144, "bfloat16"), ("ZY", 144, "bfloat16"),
+    ("ZZ", 144, "bfloat16"), ("ZL", 144, "bfloat16"), ("ID", 128, "bfloat16"), ("BK", 128, "float16"), ("JJ", L, "float16"),
+    ("IZ", 272, "bfloat16"), ("ZV", L, "bfloat16"), ("SW", 1056, "bfloat16"), ("SC", 34, "float32"), ("ST", 64, "float32"), ("KP", 32, "float32"),
+    ("PF", 128, "float32"), ("SF", 16, "float32"), ("S16", 16, "float16"), ("UX", L, "float16"), ("G", L, "float32"),
+    ("EK", 2 * L, "float32"), ("EK2", 2 * L, "float32"), ("e", 32, "float32"), ("UU", 144, "uint16"),
+    ("cvS", 256, "float32"), ("cvI", 512, "float32"), ("cvU", 128, "float32"), ("cvC", 128, "float32"),
+    ("tr", 384, "float32"), ("f", 384, "float32"), ("h", 256, "float32"), ("n", 128, "int32"), ("u", 128, "uint16"),
+    ("OW", 24, "float32"), ("MK", L, "bfloat16"), ("OG", L, "float16"), ("AC", L, "bfloat16"), ("YC", 48, "float32"),
+    ("YP", 128, "float32"), ("P0", 128, "uint16"),
+]:
+    _sb(_n, _c, _d)
+for _t in range(R):
+    for _n, _c, _d in [("sS", 256, "uint16"), ("sI", 512 if MERGE else 256, "uint16"), ("lS", 224, "uint16"),
+                       ("lI", 448 if MERGE else 224, "uint16"),
+                       ("sB", 4, "int32"), ("lB", 16, "int32"), ("sU", 16, "uint16"), ("lU", 112, "uint16"),
+                       ("sC", 128, "uint16"), ("lC", 112, "uint16"), ("sF", 8, "uint16"), ("lF", 16, "uint16")]:
+        _sb("%s%d" % (_n, _t), _c, _d)
+    _sb("P%d" % (_t + 1), 128, "uint16")
+for _b in range(8):
+    SCRATCH["ps%d" % _b] = ("psum", [128, 512], "float32")
+
+SEMAPHORES = (["qV", "qS", "qP", "qG", "sent"] + ["d%d" % i for i in range(16)]
+              + ["%s%d" % (x, t) for x in ("aF", "aS", "aI", "aB", "aU", "aC", "aD") for t in range(R)])
+
+
+def rank_program(g, core, T, topo):
+    r = T.rank_of(core)
+    if r is None:
+        return
+    eng = {"V": g.vector, "S": g.scalar, "P": g.tensor, "G": g, "Y": g.sync}
+    cnt = {"V": 0, "S": 0, "P": 0, "G": 0}
+    known = {q: {} for q in eng}
+    hist = {}
+    totals = {}
+    ndma = [0]
+
+    def A(name, lo=0, hi=None, step=1):
+        if hi is None:
+            hi = SCRATCH[name][1][1]
+        ap = T[name][:, lo:hi] if step == 1 else T[name][:, lo:hi:step]
+        return (ap, [(name, lo, hi)])
+
+    def I(win, off):
+        return (win[0].indirect(off[0]), win[1] + off[1])
+
+    def wait(q, sem, val):
+        if known[q].get(sem, 0) < val:
+            eng[q].wait_ge(T.sem[sem], val)
+            known[q][sem] = val
+
+    def order(q, reads, writes, mark, dma=False):
+        need = {}
+        acc = [(k, False) for k in reads] + [(k, True) for k in writes]
+        for (name, lo, hi), wr in acc:
+            psum = name.startswith("ps")
+            for (l2, h2, w2, q2, s2, v2) in hist.get(name, []):
+                if q2 == q and not dma:
+                    if q == "P" or wr or not w2 or h2 <= lo or hi <= l2:
+                        continue
+                elif not psum and (h2 <= lo or hi <= l2 or not (wr or w2)):
+                    continue
+                need[s2] = max(need.get(s2, 0), v2)
+        for s2 in need:
+            wait(q, s2, need[s2])
+        for (name, lo, hi), wr in acc:
+            hist.setdefault(name, []).append((lo, hi, wr, "dma" if dma else q, mark[0], mark[1]))
+
+    def op(q, fn, out, ins, more=()):
+        cnt[q] += 1
+        reads = [k for a in ins if isinstance(a, tuple) for k in a[1]] + out[1][1:]
+        order(q, reads, out[1][:1] + list(more), ("q" + q, cnt[q]))
+        fn().then_inc(T.sem["q" + q], 1)
+
+    def ap(x):
+        return x[0] if isinstance(x, tuple) else x
+
+    def copy(out, a):
+        op("V", lambda: g.vector.tensor_copy(out[0], a[0]), out, [a])
+
+    def tt(out, a, b, o):
+        op("V", lambda: g.vector.tensor_tensor(out[0], a[0], b[0], o), out, [a, b])
+
+    def ts(out, a, s1, o0, s2=None, o1=None):
+        if o1 is None:
+            op("V", lambda: g.vector.tensor_scalar(out[0], a[0], ap(s1), None, o0), out, [a, s1])
+        else:
+            op("V", lambda: g.vector.tensor_scalar(out[0], a[0], ap(s1), ap(s2), o0, o1), out, [a, s1, s2])
+
+    def red(out, a, o):
+        op("V", lambda: g.vector.tensor_reduce(out[0], a[0], AxisListType.X, o), out, [a])
+
+    def fill(out, v):
+        op("V", lambda: g.vector.memset(out[0], v), out, [])
+
+    def act(out, a, fn=AF.Copy, bias=None, scale=None, acc=None):
+        kw = {}
+        if bias is not None:
+            kw["bias"] = ap(bias)
+        if scale is not None:
+            kw["scale"] = ap(scale)
+        if acc is not None:
+            kw["accum_out"] = acc[0]
+        op("S", lambda: g.scalar.activation(out[0], a[0], fn, **kw), out, [a, bias, scale], acc[1] if acc else ())
+
+    def mm(out, lhs, rhs, start, stop):
+        op("P", lambda: g.tensor.matmul(out[0], lhs[0], rhs[0], start, stop), out, [lhs, rhs])
+
+    def iota(out, pattern, base, mult):
+        if SCRATCH[out[1][0][0]][2] == "int32":
+            op("G", lambda: g.iota(out[0], pattern, base, mult), out, [])
+        else:
+            op("G", lambda: g.iota(out[0], pattern, base, mult, allow_small_or_imprecise_dtypes=True), out, [])
+
+    def dma(q, out, a, sem=None, val=None):
+        if sem is None:
+            sem, val = "d%d" % ndma[0], 16
+            ndma[0] += 1
+        order(q, a[1], out[1], (sem, val), dma=True)
+        eng[q].dma_start(out[0], a[0]).then_inc(T.sem[sem], 16)
+        totals[sem] = val
+
+    def conv(out, z, src, blocks=range(16)):
+        for i in blocks:
+            mm(out, A(z, 15 - i, 143 - i), src(i), i == 0, i == 15)
+
+    peers = [d for d in range(N) if d != r]
+    lanes = topo.engines(core, T.cores[peers[0]])
+    far = [d for d in peers if topo.die(T.cores[d]) != topo.die(core)]
+    near = [d for d in peers if d not in far]
+    masks = {}
+    for group, pool in ((far, lanes[0::2]), (near, lanes[1::2])):
+        for i, d in enumerate(group):
+            masks[d] = (1 << pool[2 * i]) | (1 << pool[2 * i + 1])
+    totals["sent"] = 0
+
+    def dst(d):
+        rid, pid, _ = topo.addr(T.cores[d])
+        return DstId(rid=rid, pnc=pid)
+
+    def slot(d):
+        return (r - d - 1) % N
+
+    def landed(sem, val, keys):
+        totals[sem] = val
+        for name, lo, hi in keys:
+            hist.setdefault(name, []).append((lo, hi, True, "dma", sem, val))
+
+    def deal(sem, src, land, w):
+        order("G", A(src)[1], [], ("sent", 0), dma=True)
+        g.remote_dma_fused([RemoteDMATransfer(dst_ids=[dst(d)], dma_engine_mask=masks[d], remote_sem=T.sem[sem],
+                                              src=A(src, w * d, w * d + w)[0], dst=A(land, w * slot(d), w * slot(d) + w)[0])
+                            for d in peers], local_sem=T.sem.sent)
+        totals["sent"] += 2 * len(peers)
+        landed(sem, 2 * len(peers), A(land)[1])
+
+    def share(sem, src, land, keys, own=None):
+        order("G", src[1], [], ("sent", 0), dma=True)
+        g.remote_dma_fused([RemoteDMATransfer(dst_ids=[dst(d) for d in peers], dma_engine_mask=topo.mask(core, T.cores[peers[0]]),
+                                              remote_sem=T.sem[sem], srcs=[src[0]], dsts=[land(d)[0] for d in peers])],
+                           local_sem=T.sem.sent)
+        totals["sent"] += len(lanes)
+        n = len(lanes) * len(peers)
+        if own:
+            n += 16
+            dma("Y", own, src, sem, n)
+        landed(sem, n, keys)
+
+    def tree(out, cv, land, w, scale=None):
+        if scale:
+            ts(A(cv, 0, 7 * w), A(land), scale, OP.mult)
+        else:
+            copy(A(cv, 0, 7 * w), A(land))
+        tt(A("tr", 0, 4 * w), A(cv, 0, 4 * w), A(cv, 4 * w, 8 * w), OP.add)
+        tt(A("tr", 4 * w, 6 * w), A("tr", 0, 2 * w), A("tr", 2 * w, 4 * w), OP.add)
+        tt(out, A("tr", 4 * w, 5 * w), A("tr", 5 * w, 6 * w), OP.add)
+
+    def ext(t):
+        return (t, [])
+
+    def expand(t):
+        for k in range(16):
+            act(A("XE%d" % t, k, 4096, 16), A("X", L * t, L * t + L))
+
+    def clear_window():
+        act(A("W1"), A("XE0", 0, W), AF.Identity, scale=0.0)
+
+    dma("Y", A("PA"), ext(T.pa[:]))
+    dma("Y", A("X", 0, L), ext(T.xv[:, 0:L]))
+    dma("S", A("BC", 0, Q), ext(T.bt[:]))
+    dma("S", A("BC", Q, 2 * Q), ext(T.co[:]))
+    dma("Y", A("CD"), ext(T.cd[:]))
+    dma("Y", A("K"), ext(T.kc[:]))
+    dma("Y", A("X", L, V), ext(T.xv[:, L:V]))
+
+    cA, cG, c15, cT, cW, cC, cZ, cU, cV = [A("col", i, i + 1) for i in range(9)]
+    row6, row7 = A("I16", 6, 7), A("I16", 7, 8)
+    BN, DN, VN, ZS = A("ST", 0, 2), A("ST", 2, 4), A("ST", 16, 32), A("ST", 32, 48)
+    iota(A("ii", 0, 1), [[0, 1]], 0, 1)
+    iota(A("i1"), [[1, 144]], 0, -1)
+    iota(A("i3"), [[0, 16], [1, 16]], 0, 0)
+    iota(A("i4"), [[1, 16], [0, 16]], 0, 0)
+    iota(A("i5"), [[1, 256]], 0, 0)
+    iota(A("KP"), [[0, 2], [1, 16]], 0, 0)
+    iota(A("CP", 6 * Q, 7 * Q), [[1, Q]], -Q // 2, 0)
+    iota(A("META", 0, C // 3), [[0, C // 3]], 1, 0)
+    fill(A("META", C // 3, 2 * C // 3), 1.0)
+    act(A("META", 2 * C // 3, C), A("META", C // 3, 2 * C // 3))
+    ts(A("ii", 1, 2), A("ii", 0, 1), 15, OP.bitwise_and)
+    ts(A("ii", 2, 3), A("ii", 0, 1), 4, OP.arith_shift_right)
+    copy(A("col", 0, 2), A("ii", 1, 3))
+    ts(c15, cA, -1.0, OP.mult, 15.0, OP.add)
+    ts(A("I16"), A("i3", 0, 16), cA, OP.is_equal)
+    ts(A("BK"), A("i4", 0, 128), cG, OP.is_equal)
+    ts(A("ZA"), A("i1"), c15, OP.is_equal)
+    ts(A("ID"), A("i1", 0, 128), 0.0, OP.is_equal)
+    ts(A("JJ"), A("i5"), A("I16", 0, 1), OP.mult, 1.0 / 512, OP.mult)
+    ts(VN, A("i3", 0, 16), 16.0, OP.mult, cA, OP.add)
+    for a in range(16):
+        ts(A("BA", 128 * a, 128 * a + 128), A("BK"), A("I16", a, a + 1), OP.mult)
+    ts(BN, A("ST", 16 + 2 * r, 18 + 2 * r), -1.0 / 512, OP.mult, 0.25, OP.add)
+    ts(DN, A("ST", 16 + 2 * r, 18 + 2 * r), float(V), OP.add)
+    copy(A("P0"), A("PA"))
+
+    def own_lane(i, a):
+        return A("e", 2 * i + a, 2 * i + a + 1)
+
+    def first_keys(t):
+        s = A("P%d" % t, 16 * t, 16 * t + 16)
+        copy(A("S16"), s)
+        copy(A("SF"), s)
+        mm(A("ps4", 0, 256), A("BK"), A("JJ"), True, False)
+        for a in range(16):
+            mm(A("ps4", a, 256, 16), A("BA", 128 * a, 128 * a + 128), A("S16"), False, a == 15)
+
+    def first_slots(t):
+        sf = [A("SF", 2 * r + a, 2 * r + a + 1) for a in range(2)]
+        for a in range(2):
+            act(own_lane(0, a), sf[a], AF.Identity, bias=A("ST", a, a + 1), scale=-1.0)
+        act(A("e", 2, 4), A("SF", 2 * r, 2 * r + 2), AF.Abs, bias=-(L * t + 127.5))
+        for a in range(2):
+            act(A("EK", L * a, L * a + L), A("ps4", 0, 256), AF.Abs, bias=own_lane(0, a))
+        act(A("e", 4, 6), A("e", 2, 4), AF.Relu, bias=128.0, scale=-1.0)
+        for a in range(2):
+            act(A("EK2", L * a, L * a + L), A("EK", L * a, L * a + L), AF.Relu, bias=0.249, scale=-1.0, acc=own_lane(3, a))
+        for a in range(2):
+            act(own_lane(4, a), sf[a], AF.Identity, bias=A("ST", 2 + a, 3 + a), scale=-1.0)
+        for a in range(2):
+            act(own_lane(5, a), own_lane(3, a), AF.Sign, bias=own_lane(2, a))
+        for a in range(2):
+            act(own_lane(6, a), own_lane(5, a), AF.Identity, bias=sf[a], scale=own_lane(4, a))
+
+    def first_send(t):
+        src, place = A("sF%d" % t, 0, 2), A("lF%d" % t, 2 * r, 2 * r + 2)
+        copy(src, A("e", 12, 14))
+        share("aF%d" % t, src, lambda d: place, A("lF%d" % t)[1], place)
+
+    first_keys(0)
+    first_slots(0)
+    expand(0)
+    copy(A("CP", 0, 2 * Q), A("BC"))
+    ts(cU, cA, float(Q), OP.mult, Q / 2, OP.add)
+    tt(A("BR"), A("BC"), A("CP", 0, 2 * Q), OP.subtract)
+    first_send(0)
+    copy(A("CP", 2 * Q, 4 * Q), A("BR"))
+    ts(A("CP", 7 * Q, 8 * Q), A("CP", 6 * Q, 7 * Q), 0.0, OP.mult, cU, OP.add)
+    tt(A("CP", 4 * Q, 6 * Q), A("BR"), A("CP", 2 * Q, 4 * Q), OP.subtract)
+    msem = "d%d" % ndma[0]
+    ndma[0] += 1
+    order("Y", A("CP")[1] + A("K")[1], A("META")[1], (msem, 128), dma=True)
+    for row, part in ((0, 0), (1, 2), (2, 4), (3, 1), (4, 3), (5, 5), (6, 6), (8, 7)):
+        g.sync.dma_start(T.META[row:128:16, :], T.CP[:, part * Q:part * Q + Q]).then_inc(T.sem[msem], 16)
+    totals[msem] = 128
+    red(cT, A("I16", 0, 3), OP.add)
+    red(cW, A("I16", 3, 6), OP.add)
+    tt(cC, A("I16", 8, 9), row6, OP.add)
+    ts(A("ZT"), A("i1"), c15, OP.is_equal, cT, OP.mult)
+    ts(A("ZW"), A("i1"), c15, OP.is_equal, cW, OP.mult)
+    ts(A("ZC"), A("i1"), c15, OP.is_equal, cC, OP.mult)
+
+    def window_constants():
+        ts(cU, row6, -15.0, OP.mult, 16.0, OP.add)
+        ts(cV, row6, 15.0, OP.mult, 1.0, OP.add)
+        ts(A("EK", 0, L), A("i3"), cU, OP.mult, 1.0, OP.add)
+        ts(A("EK", L, 2 * L), A("i4"), cV, OP.mult)
+        tt(A("ZV"), A("EK", 0, L), A("EK", L, 2 * L), OP.add)
+        ts(A("KP"), A("KP"), 16384.0, OP.mult)
+
+    tt(cZ, cW, row7, OP.add)
+    for name in ("IZ", "KC", "MB", "SB", "OW"):
+        iota(A(name, 0, 16), [[0, 16]], 0, 0)
+    iota(A("SC"), [[0, 34]], 2 ** 22, 0)
+    iota(A("SW", 0, 2), [[2, 2]], -1, 0)
+    iota(A("SW", 2, 16), [[0, 14]], 0, 0)
+    iota(A("SW", 16, 18), [[0, 2]], 1, 0)
+    iota(A("SW", 18, 1056), [[0, 1038]], 0, 0)
+
+    def last_constants():
+        ts(A("ZY"), A("i1"), c15, OP.is_equal, row7, OP.mult)
+        ts(A("ZL"), A("i1"), c15, OP.is_equal, row6, OP.mult)
+        ts(A("IZ", 16, 272), A("i3"), cA, OP.is_equal)
+        ts(A("ZZ"), A("i1"), c15, OP.is_equal, cZ, OP.mult)
+        ts(cU, cA, 16.0, OP.mult, 1.0, OP.add)
+        ts(ZS, A("i3", 0, 16), cU, OP.add)
+        ts(VN, VN, float(L * r), OP.add)
+
+    for t in range(R):
+        P, Pn = "P%d" % t, "P%d" % (t + 1)
+        s = A(P, 16 * t, 16 * t + 16)
+        XE = "XE%d" % t
+        pX, pI, pS = A("ps0", 0, 256), A("ps1", 0, 256), A("ps2", 0, 256)
+
+        def parents_x():
+            act(A("XS"), I(A("X"), s))
+            mm(pX, A("ID"), A("XS"), True, True)
+
+        def own_side(lo, hi):
+            tt(A("PI", 16 * lo, 16 * hi), I(A("K"), A("E", lo, hi)), A(XE, 16 * lo, 16 * hi), OP.mult)
+            conv(pI, "ZA", lambda b: A("PI", 256 * b, 256 * b + 256), range(lo // 16, hi // 16))
+
+        spare = ("ps3", "ps5", "ps6", "ps7")
+        for j, bank in enumerate(spare):
+            mm(A(bank), A("ID"), A(XE, 2048 + 512 * j, 2560 + 512 * j), True, True)
+        copy(A("E"), I(A("CD"), s))
+        if t:
+            parents_x()
+        act(A("KG", 0, 2048), I(A("K"), A("E", 0, 128)))
+        if not t:
+            parents_x()
+        act(A("KG", 2048, 4096), I(A("K"), A("E", 128, 256)))
+        own_side(0, 64)
+        if t:
+            first_keys(t)
+            first_slots(t)
+        own_side(64, 128)
+        for a in range(2):
+            copy(A("EO", a, 32, 2), A("E", 2 * r + a, L, 16))
+        act(A("MG"), I(A("META"), A("EO")))
+        if not t:
+            clear_window()
+        for h in range(2):
+            for k in range(16):
+                tt(A("PS", 2048 * h + k, 2048 * h + 2048, 16), A("KG", 2048 * h + k, 2048 * h + 2048, 16),
+                   A("ps0", 128 * h, 128 * h + 128), OP.mult)
+            conv(pS, "ZA", lambda b: A("PS", 256 * b, 256 * b + 256), range(8 * h, 8 * h + 8))
+        if t:
+            first_send(t)
+        for j, bank in enumerate(spare):
+            cuts = (0, 512) if j < 3 else (0, 256, 512)
+            for lo, hi in zip(cuts, cuts[1:]):
+                c0 = 2048 + 512 * j
+                tt(A("PI", c0 + lo, c0 + hi), A("KG", c0 + lo, c0 + hi), A(bank, lo, hi), OP.mult)
+                conv(pI, "ZA", lambda b: A("PI", 256 * b, 256 * b + 256), range((c0 + lo) // 256, (c0 + hi) // 256))
+            if j == 1 and not MERGE:
+                ts(A("sS%d" % t), pS, BIAS, OP.add)
+                deal("aS%d" % t, "sS%d" % t, "lS%d" % t, 32)
+        if MERGE:
+            ts(A("sI%d" % t, 0, 512, 2), pS, BIAS, OP.add)
+            ts(A("sI%d" % t, 1, 512, 2), pI, BIAS, OP.add)
+            deal("aI%d" % t, "sI%d" % t, "lI%d" % t, 64)
+        else:
+            ts(A("sI%d" % t), pI, BIAS, OP.add)
+            deal("aI%d" % t, "sI%d" % t, "lI%d" % t, 32)
+
+        thr, pay, dS, dI, sc, tq, uq = [A("f", 32 * i, 32 * i + 32) for i in range(7)]
+        mcol = lambda i: A("f", 256 + i, 257 + i)
+        conv(A("ps3", 0, 32), "ZT", lambda b: A("MG", 32 * b, 32 * b + 32))
+        conv(A("ps0", 0, 32), "ZW", lambda b: A("MG", 32 * b, 32 * b + 32))
+        conv(A("ps0", 32, 64), "ZC", lambda b: A("MG", 32 * b, 32 * b + 32))
+        cu, fo, sh, sl, upu, ao = [A("u", 16 * i, 16 * i + 16) for i in range(6)]
+        n0, n1, n2, n3, n4 = [A("n", 16 * i, 16 * i + 16) for i in range(5)]
+        if not t:
+            window_constants()
+        copy(n0, s)
+        copy(A("PF"), A(P))
+        ts(n1, n0, 4, OP.arith_shift_right)
+        ts(n2, n0, 15, OP.bitwise_and)
+        copy(sh, n1)
+        copy(sl, n2)
+        act(A("G"), I(A("PF"), sh))
+        copy(I(A("W1"), A("lF%d" % t)), A("ZV"))
+        act(A("UB", V, W), A("W1", L * r, L * r + L))
+        act(A("UB", 0, V), I(A("W1"), A(P)))
+        ts(thr, A("ps3", 0, 32), 7 * BIAS + 0.5, OP.add)
+        if MERGE:
+            tt(A("f", 288, 352, 2), A("ps2", 32 * r, 32 * r + 32), thr, OP.subtract)
+            tt(A("f", 289, 352, 2), A("ps1", 32 * r, 32 * r + 32), thr, OP.subtract)
+            tt(sc, A("KP"), A("ps0", 32, 64), OP.add)
+            ts(A("cvI", 448, 512), A("f", 288, 352), 2.0 ** 13, OP.mult)
+        else:
+            tt(A("cvS", 224, 256), A("ps2", 32 * r, 32 * r + 32), thr, OP.subtract)
+            tt(A("cvI", 224, 256), A("ps1", 32 * r, 32 * r + 32), thr, OP.subtract)
+            tree(dS, "cvS", "lS%d" % t, 32)
+            tt(sc, A("KP"), A("ps0", 32, 64), OP.add)
+            ts(pay, dS, 0.0, OP.is_lt, 8192.0, OP.mult)
+            ts(dS, dS, 2.0 ** 26, OP.mult)
+            tt(pay, pay, sc, OP.add)
+        tt(A("UX"), I(A("I16"), sl), A("G"), OP.mult)
+        conv(A("ps4", 64, 80), "ZA", lambda b: A("UX", 16 * b, 16 * b + 16))
+        if r == t:
+            conv(A("ps4", 16, 32), "ZA", lambda a: A("UX", a, L, 16))
+        for b in range(2):
+            mm(A("ps%d" % (1 + b)), A("ID"), A("X", 512 + 512 * b, 1024 + 512 * b), True, True)
+
+        if MERGE:
+            ts(A("ps6", 0, 256), A("lI%d" % t, 0, 256), 2.0 ** 13, OP.mult)
+            ts(A("cvI", 256, 448), A("lI%d" % t, 256, 448), 2.0 ** 13, OP.mult)
+            tt(A("ps7", 0, 128), A("ps6", 0, 128), A("cvI", 256, 384), OP.add)
+            tt(A("tr", 0, 128), A("ps6", 128, 256), A("cvI", 384, 512), OP.add)
+            tt(A("tr", 128, 256), A("ps7", 0, 128), A("tr", 0, 128), OP.add)
+            tt(A("f", 64, 128), A("tr", 128, 192), A("tr", 192, 256), OP.add)
+            tt(tq, A("f", 64, 128, 2), A("f", 65, 128, 2), OP.mult)
+            ts(pay, A("f", 64, 128, 2), 0.0, OP.is_lt, 8192.0, OP.mult)
+            tt(A("SC", 1, 33), tq, A("ps0", 0, 32), OP.max)
+            tt(pay, pay, sc, OP.add)
+        else:
+            tree(dI, "cvI", "lI%d" % t, 32)
+            tt(dI, dI, dS, OP.mult)
+            tt(A("SC", 1, 33), dI, A("ps0", 0, 32), OP.max)
+        for a in range(2):
+            red(mcol(a), A("SC", 17 * a, 17 * a + 17), OP.min)
+        for a in range(2):
+            ts(A("f", 160 + 16 * a, 176 + 16 * a), A("SC", 1 + 16 * a, 17 + 16 * a), mcol(a), OP.is_gt, 2.0 ** 23, OP.mult)
+        tt(uq, tq, pay, OP.add)
+        for a in range(2):
+            red(A("sB%d" % t, a, a + 1), A("f", 192 + 16 * a, 208 + 16 * a), OP.min)
+        msg, lB = A("sB%d" % t, 0, 2), A("lB%d" % t)
+        place = A("lB%d" % t, 2 * r, 2 * r + 2)
+        share("aB%d" % t, msg, lambda d: place, lB[1], place)
+
+        thJ = A("h", 0, 32)
+        okN, e1, e2, val, base, ya, dl, dU, dC = [A("h", 32 + 16 * i, 48 + 16 * i) for i in range(9)]
+        Po = A("PF", 16 * r, 16 * r + 16)
+        copy(upu, A("ps4", 64, 80))
+        if not t:
+            last_constants()
+        conv(A("ps5", 0, 144), "ZY", lambda a: A("UB", a, W, 16))
+        act(A("XS"), I(A("X"), upu))
+        ts(okN, A("lF%d" % t), float(V), OP.is_lt)
+        if r == t:
+            tt(e2, ZS, okN, OP.mult)
+            ts(A("UU", 0, 128), A("ps5", 0, 128), 15.0, OP.add)
+            ts(A("UU", 128, 144), e2, 15.0, OP.add)
+            ts(n3, e2, 15.0, OP.add)
+        else:
+            ts(A("UU"), A("ps5", 0, 144), 15.0, OP.add)
+            ts(n3, A("ps5", 128, 144), 15.0, OP.add)
+        mm(A("ps6", 256, 512), A("ID"), A("XS"), True, True)
+        mm(A("ps0"), A("ID"), A("X", 1536, 2048), True, True)
+        conv(A("ps4", 0, 16), "ZL", lambda a: A("UB", L * r + a, L * r + L, 16))
+        if r != t:
+            conv(A("ps4", 16, 32), "ZL", lambda a: A("UB", V + a, W, 16))
+        act(A("MK"), I(A("IZ"), A("UU", 128, 144)))
+        ts(n4, n3, 4, OP.arith_shift_right)
+        copy(ao, n4)
+
+        ts(n0, lB, 8191, OP.bitwise_and)
+        ts(n1, lB, 13, OP.arith_shift_right, 1025, OP.bitwise_and)
+        copy(cu, n0)
+        copy(A("KC", 16, 272), I(A("K"), cu))
+        for b in range(3):
+            act(A("KA", 512 * b, 512 * b + 512), I(A("KC"), A("UU", 32 + 32 * b, 64 + 32 * b)))
+        tt(A("PU"), A("KC", 16, 272), A("ps6", 256, 512), OP.mult)
+        conv(A("ps6", 0, 16), "ZA", lambda b: A("PU", b, L, 16))
+        tt(A("PC", 0, 512), I(A("KC"), A("UU", 0, 32)), A("X", 0, 512), OP.mult)
+        ts(A("sU%d" % t), A("ps6", 0, 16), BIAS, OP.add)
+        share("aU%d" % t, A("sU%d" % t), lambda d: A("lU%d" % t, 16 * slot(d), 16 * slot(d) + 16), A("lU%d" % t)[1])
+        copy(fo, n1)
+        for b in range(3):
+            tt(A("PC", 512 + 512 * b, 1024 + 512 * b), A("KA", 512 * b, 512 * b + 512), A(("ps1", "ps2", "ps0")[b]), OP.mult)
+            if not b:
+                conv(A("ps7", 0, 64), "ZA", lambda a: A("PC", a, 1024, 16))
+        conv(A("ps7", 64, 128), "ZA", lambda a: A("PC", 1024 + a, V, 16))
+        mine_u = A("UU", 16 * r, 16 * r + 16)
+        act(A("MB", 16, 272), I(A("META"), cu))
+        act(A("SB", 16, 272), I(A("SW", 0, 1040), fo))
+        act(A("MB", 272, 528), I(A("MB", 0, 272), mine_u))
+        act(A("SB", 272, 528), I(A("SB", 0, 272), mine_u))
+        ts(e1, A("ps4", 0, 16), float(L * t - 1), OP.add)
+        if r == t:
+            tt(val, A("ps4", 16, 32), Po, OP.subtract)
+        else:
+            ts(e2, A("ps4", 16, 32), float(L * t - 1), OP.add)
+        ts(A("sC%d" % t), A("ps7", 0, 128), BIAS, OP.add)
+        deal("aC%d" % t, "sC%d" % t, "lC%d" % t, 16)
+
+        conv(A("ps3", 0, 32), "ZT", lambda a: A("MB", 16 + a, 528, 16))
+        conv(A("ps4", 32, 64), "ZY", lambda a: A("SB", 16 + a, 528, 16))
+        if t + 1 < R:
+            clear_window()
+            expand(t + 1)
+        tt(dl, e1, Po, OP.subtract)
+        if r == t:
+            tt(e2, e1, VN, OP.not_equal)
+            tt(dl, dl, e2, OP.mult)
+        else:
+            tt(val, e2, Po, OP.subtract)
+        ts(thJ, A("ps3", 0, 32), 7 * BIAS + 0.5, OP.add)
+        tt(A("cvU", 112, 128), A("ps6", 0, 16), A("h", 0, 16), OP.subtract)
+        tt(A("cvC", 112, 128), A("ps7", 16 * r, 16 * r + 16), A("h", 16, 32), OP.subtract)
+        tree(dU, "cvU", "lU%d" % t, 16)
+        tt(dU, dU, A("ps4", 32, 48), OP.mult)
+        ts(A("OW", 1, 17), dU, 0.0, OP.is_gt)
+        tt(A("OG"), I(A("OW", 0, 17), ao), A("MK"), OP.mult)
+        conv(A("ps6", 16, 32), "ZA", lambda a: A("OG", a, L, 16))
+        ts(ya, A("ps6", 16, 32), 0.5, OP.is_lt)
+        tt(base, A("ps6", 16, 32), val, OP.mult)
+        tt(ya, ya, A("ps4", 48, 64), OP.mult)
+        tt(base, base, Po, OP.add)
+
+        tree(dC, "cvC", "lC%d" % t, 16)
+        tt(dC, dC, ya, OP.mult)
+        ts(dC, dC, 0.0, OP.is_gt)
+        tt(dC, dC, dl, OP.mult)
+        tt(dC, dC, base, OP.add)
+        mine = A(Pn, 16 * r, 16 * r + 16)
+        copy(mine, dC)
+        share("aD%d" % t, mine, lambda d: mine, [(Pn, 16 * d, 16 * d + 16) for d in peers])
+
+        tt(A("AC"), I(A("SW", 16, 1056), fo), A("MB", 16, 272), OP.mult)
+        conv(A("ps3", 64, 80), "ZZ", lambda a: A("AC", 16 * a, 16 * a + 16))
+        tt(e1, A("ps3", 64, 80), okN, OP.mult)
+        ts(A("YC", 16 * t, 16 * t + 16), e1, -1.0, OP.add)
+
+    dma("S", ext(T.yc[:]), A("YC"))
+    copy(A("YP"), A("P%d" % R))
+    dma("Y", ext(T.yp[:]), A("YP"))
+    for q in cnt:
+        totals["q" + q] = cnt[q]
+    for sem in sorted(totals, key=lambda x: x[0] == "d"):
+        if all(known[q].get(sem, 0) < totals[sem] for q in eng):
+            wait("G", sem, totals[sem])

@@ -18,14 +18,14 @@ for _n, _c, _d in [
     ("K", C, "bfloat16"), ("X", V, "bfloat16"), ("CD", V, "int32"), ("PA", 128, "int32"), ("META", C, "bfloat16"),
     ("BC", 2 * Q, "int32"), ("BR", 2 * Q, "float32"), ("CP", 8 * Q, "bfloat16"),
     ("W1", W, "bfloat16"), ("UB", W, "bfloat16"), ("KG", 4096, "bfloat16"), ("PI", 4096, "float16"), ("PS", 4096, "float16"),
-    ("XE0", 4096, "bfloat16"), ("XE1", 4096, "bfloat16"), ("XE2", 4096, "bfloat16"), ("BA", 2048, "float16"),
+    ("XE0", 2048, "bfloat16"), ("XE1", 2048, "bfloat16"), ("XE2", 2048, "bfloat16"), ("BA", 2048, "float16"),
     ("PC", V, "float16"), ("PU", L, "float16"), ("XS", L, "bfloat16"), ("KC", 272, "bfloat16"), ("KA", 1536, "bfloat16"),
     ("MB", 528, "bfloat16"), ("SB", 528, "bfloat16"), ("MG", 512, "bfloat16"), ("E", L, "uint16"), ("EO", 32, "uint16"),
     ("i1", 144, "float32"), ("i3", 256, "float32"), ("i4", 256, "float32"), ("i5", 256, "float32"),
     ("ii", 32, "int32"), ("col", 32, "float32"), ("I16", 16, "float32"),
     ("ZA", 144, "float16"), ("ZT", 144, "bfloat16"), ("ZW", 144, "bfloat16"), ("ZC", 144, "bfloat16"), ("ZY", 144, "bfloat16"),
     ("ZZ", 144, "bfloat16"), ("ZL", 144, "bfloat16"), ("ID", 128, "bfloat16"), ("BK", 128, "float16"), ("JJ", L, "float16"),
-    ("IZ", 272, "bfloat16"), ("ZV", L, "bfloat16"), ("SW", 1056, "bfloat16"), ("SC", 34, "float32"), ("ST", 64, "float32"), ("KP", 32, "float32"),
+    ("IZ", 272, "bfloat16"), ("ZV", L, "bfloat16"), ("SW", 1056, "bfloat16"), ("SC", 34, "float32"), ("ST", 64, "float32"), ("KP", 32, "bfloat16"),
     ("PF", 128, "float32"), ("SF", 16, "float32"), ("S16", 16, "float16"), ("UX", L, "float16"), ("G", L, "float32"),
     ("EK", 2 * L, "float32"), ("EK2", 2 * L, "float32"), ("e", 32, "float32"), ("UU", 144, "uint16"),
     ("cvS", 256, "float32"), ("cvI", 512, "float32"), ("cvU", 128, "float32"), ("cvC", 128, "float32"),
@@ -204,10 +204,10 @@ def rank_program(g, core, T, topo):
 
     def expand(t):
         for k in range(16):
-            act(A("XE%d" % t, k, 4096, 16), A("X", L * t, L * t + L))
+            act(A("XE%d" % t, k, 2048, 16), A("X", L * t, L * t + 128))
 
     def clear_window():
-        act(A("W1"), A("XE0", 0, W), AF.Identity, scale=0.0)
+        iota(A("W1"), [[0, W]], 0, 0)
 
     dma("Y", A("PA"), ext(T.pa[:]))
     dma("Y", A("X", 0, L), ext(T.xv[:, 0:L]))
@@ -225,7 +225,7 @@ def rank_program(g, core, T, topo):
     iota(A("i3"), [[0, 16], [1, 16]], 0, 0)
     iota(A("i4"), [[1, 16], [0, 16]], 0, 0)
     iota(A("i5"), [[1, 256]], 0, 0)
-    iota(A("KP"), [[0, 2], [1, 16]], 0, 0)
+    iota(A("KP"), [[0, 2], [16384, 16]], 0, 0)
     iota(A("CP", 6 * Q, 7 * Q), [[1, Q]], -Q // 2, 0)
     iota(A("META", 0, C // 3), [[0, C // 3]], 1, 0)
     fill(A("META", C // 3, 2 * C // 3), 1.0)
@@ -284,49 +284,52 @@ def rank_program(g, core, T, topo):
     expand(0)
     copy(A("CP", 0, 2 * Q), A("BC"))
     ts(cU, cA, float(Q), OP.mult, Q / 2, OP.add)
-    tt(A("BR"), A("BC"), A("CP", 0, 2 * Q), OP.subtract)
+    for i in range(2):
+        tt(A("ps%d" % (1 + i), 0, Q), A("BC", i * Q, i * Q + Q), A("CP", i * Q, i * Q + Q), OP.subtract)
     first_send(0)
-    copy(A("CP", 2 * Q, 4 * Q), A("BR"))
+    for i in range(2):
+        copy(A("CP", (2 + i) * Q, (3 + i) * Q), A("ps%d" % (1 + i), 0, Q))
     ts(A("CP", 7 * Q, 8 * Q), A("CP", 6 * Q, 7 * Q), 0.0, OP.mult, cU, OP.add)
-    tt(A("CP", 4 * Q, 6 * Q), A("BR"), A("CP", 2 * Q, 4 * Q), OP.subtract)
+    for i in range(2):
+        tt(A("CP", (4 + i) * Q, (5 + i) * Q), A("ps%d" % (1 + i), 0, Q), A("CP", (2 + i) * Q, (3 + i) * Q), OP.subtract)
     msem = "d%d" % ndma[0]
     ndma[0] += 1
     order("Y", A("CP")[1] + A("K")[1], A("META")[1], (msem, 128), dma=True)
     for row, part in ((0, 0), (1, 2), (2, 4), (3, 1), (4, 3), (5, 5), (6, 6), (8, 7)):
         g.sync.dma_start(T.META[row:128:16, :], T.CP[:, part * Q:part * Q + Q]).then_inc(T.sem[msem], 16)
     totals[msem] = 128
-    red(cT, A("I16", 0, 3), OP.add)
-    red(cW, A("I16", 3, 6), OP.add)
-    tt(cC, A("I16", 8, 9), row6, OP.add)
-    ts(A("ZT"), A("i1"), c15, OP.is_equal, cT, OP.mult)
-    ts(A("ZW"), A("i1"), c15, OP.is_equal, cW, OP.mult)
-    ts(A("ZC"), A("i1"), c15, OP.is_equal, cC, OP.mult)
 
-    def window_constants():
-        ts(cU, row6, -15.0, OP.mult, 16.0, OP.add)
-        ts(cV, row6, 15.0, OP.mult, 1.0, OP.add)
-        ts(A("EK", 0, L), A("i3"), cU, OP.mult, 1.0, OP.add)
-        ts(A("EK", L, 2 * L), A("i4"), cV, OP.mult)
-        tt(A("ZV"), A("EK", 0, L), A("EK", L, 2 * L), OP.add)
-        ts(A("KP"), A("KP"), 16384.0, OP.mult)
+    def selectors(h):
+        if not h:
+            red(cT, A("I16", 0, 3), OP.add)
+            red(cW, A("I16", 3, 6), OP.add)
+            tt(cC, A("I16", 8, 9), row6, OP.add)
+            ts(A("ZT"), A("i1"), c15, OP.is_equal, cT, OP.mult)
+            ts(cV, cW, 2.0 ** -25, OP.mult)
+        else:
+            ts(A("ZW"), A("i1"), c15, OP.is_equal, cV, OP.mult)
+            ts(A("ZC"), A("i1"), c15, OP.is_equal, cC, OP.mult)
+            fill(A("SC"), 0.125)
 
-    tt(cZ, cW, row7, OP.add)
+    iota(A("ZV"), [[1, 16], [16, 16]], 1, 0)
+    iota(A("AC"), [[1, L]], 1, 0)
+    dma("Y", (T.ZV[6:128:16, :], A("ZV")[1]), (T.AC[6:128:16, :], A("AC")[1]))
+    clear_window()
     for name in ("IZ", "KC", "MB", "SB", "OW"):
         iota(A(name, 0, 16), [[0, 16]], 0, 0)
-    iota(A("SC"), [[0, 34]], 2 ** 22, 0)
     iota(A("SW", 0, 2), [[2, 2]], -1, 0)
     iota(A("SW", 2, 16), [[0, 14]], 0, 0)
     iota(A("SW", 16, 18), [[0, 2]], 1, 0)
     iota(A("SW", 18, 1056), [[0, 1038]], 0, 0)
 
     def last_constants():
-        ts(A("ZY"), A("i1"), c15, OP.is_equal, row7, OP.mult)
         ts(A("ZL"), A("i1"), c15, OP.is_equal, row6, OP.mult)
-        ts(A("IZ", 16, 272), A("i3"), cA, OP.is_equal)
-        ts(A("ZZ"), A("i1"), c15, OP.is_equal, cZ, OP.mult)
-        ts(cU, cA, 16.0, OP.mult, 1.0, OP.add)
-        ts(ZS, A("i3", 0, 16), cU, OP.add)
-        ts(VN, VN, float(L * r), OP.add)
+        act(A("EK", 0, L), A("i3"), AF.Abs, bias=cA, scale=-1.0)
+        act(A("IZ", 16, 272), A("EK", 0, L), AF.Relu, bias=1.0, scale=-1.0)
+        if r < R:
+            act(cU, cA, AF.Identity, bias=1.0, scale=16.0)
+            act(ZS, A("i3", 0, 16), AF.Identity, bias=cU)
+            act(VN, VN, AF.Identity, bias=float(L * r))
 
     for t in range(R):
         P, Pn = "P%d" % t, "P%d" % (t + 1)
@@ -344,7 +347,8 @@ def rank_program(g, core, T, topo):
 
         spare = ("ps3", "ps5", "ps6", "ps7")
         for j, bank in enumerate(spare):
-            mm(A(bank), A("ID"), A(XE, 2048 + 512 * j, 2560 + 512 * j), True, True)
+            for k in range(16):
+                mm(A(bank, k, 512, 16), A("ID"), A("X", L * t + 128 + 32 * j, L * t + 160 + 32 * j), True, True)
         copy(A("E"), I(A("CD"), s))
         if t:
             parents_x()
@@ -361,8 +365,12 @@ def rank_program(g, core, T, topo):
             copy(A("EO", a, 32, 2), A("E", 2 * r + a, L, 16))
         act(A("MG"), I(A("META"), A("EO")))
         if not t:
-            clear_window()
+            last_constants()
+        cu, fo, sh, sl, upu, ao = [A("u", 16 * i, 16 * i + 16) for i in range(6)]
+        n0, n1, n2, n3, n4 = [A("n", 16 * i, 16 * i + 16) for i in range(5)]
         for h in range(2):
+            if not t:
+                selectors(h)
             for k in range(16):
                 tt(A("PS", 2048 * h + k, 2048 * h + 2048, 16), A("KG", 2048 * h + k, 2048 * h + 2048, 16),
                    A("ps0", 128 * h, 128 * h + 128), OP.mult)
@@ -375,72 +383,47 @@ def rank_program(g, core, T, topo):
                 c0 = 2048 + 512 * j
                 tt(A("PI", c0 + lo, c0 + hi), A("KG", c0 + lo, c0 + hi), A(bank, lo, hi), OP.mult)
                 conv(pI, "ZA", lambda b: A("PI", 256 * b, 256 * b + 256), range((c0 + lo) // 256, (c0 + hi) // 256))
-            if j == 1 and not MERGE:
-                ts(A("sS%d" % t), pS, BIAS, OP.add)
-                deal("aS%d" % t, "sS%d" % t, "lS%d" % t, 32)
-        if MERGE:
-            ts(A("sI%d" % t, 0, 512, 2), pS, BIAS, OP.add)
-            ts(A("sI%d" % t, 1, 512, 2), pI, BIAS, OP.add)
-            deal("aI%d" % t, "sI%d" % t, "lI%d" % t, 64)
-        else:
-            ts(A("sI%d" % t), pI, BIAS, OP.add)
-            deal("aI%d" % t, "sI%d" % t, "lI%d" % t, 32)
+        ts(A("sI%d" % t, 0, 512, 2), pS, BIAS, OP.add)
+        ts(A("sI%d" % t, 1, 512, 2), pI, BIAS, OP.add)
+        deal("aI%d" % t, "sI%d" % t, "lI%d" % t, 64)
 
         thr, pay, dS, dI, sc, tq, uq = [A("f", 32 * i, 32 * i + 32) for i in range(7)]
         mcol = lambda i: A("f", 256 + i, 257 + i)
         conv(A("ps3", 0, 32), "ZT", lambda b: A("MG", 32 * b, 32 * b + 32))
         conv(A("ps0", 0, 32), "ZW", lambda b: A("MG", 32 * b, 32 * b + 32))
-        conv(A("ps0", 32, 64), "ZC", lambda b: A("MG", 32 * b, 32 * b + 32))
-        cu, fo, sh, sl, upu, ao = [A("u", 16 * i, 16 * i + 16) for i in range(6)]
-        n0, n1, n2, n3, n4 = [A("n", 16 * i, 16 * i + 16) for i in range(5)]
-        if not t:
-            window_constants()
+        conv(A("ps0", 32, 64), "ZC", lambda b: A("MG", 32 * b, 32 * b + 32), range(15))
+        mm(A("ps0", 32, 64), A("ID"), A("KP"), False, False)
+        conv(A("ps0", 32, 64), "ZC", lambda b: A("MG", 32 * b, 32 * b + 32), [15])
+        copy(I(A("W1"), A("lF%d" % t)), A("ZV"))
+        act(thr, A("ps3", 0, 32), AF.Identity, bias=7 * BIAS + 0.5)
+        act(A("UB", 0, 1280), I(A("W1"), A(P, 0, 80)))
         copy(n0, s)
         copy(A("PF"), A(P))
         ts(n1, n0, 4, OP.arith_shift_right)
         ts(n2, n0, 15, OP.bitwise_and)
+        copy(A("UB", V, W), A("W1", L * r, L * r + L))
         copy(sh, n1)
         copy(sl, n2)
-        act(A("G"), I(A("PF"), sh))
-        copy(I(A("W1"), A("lF%d" % t)), A("ZV"))
-        act(A("UB", V, W), A("W1", L * r, L * r + L))
-        act(A("UB", 0, V), I(A("W1"), A(P)))
-        ts(thr, A("ps3", 0, 32), 7 * BIAS + 0.5, OP.add)
-        if MERGE:
-            tt(A("f", 288, 352, 2), A("ps2", 32 * r, 32 * r + 32), thr, OP.subtract)
-            tt(A("f", 289, 352, 2), A("ps1", 32 * r, 32 * r + 32), thr, OP.subtract)
-            tt(sc, A("KP"), A("ps0", 32, 64), OP.add)
-            ts(A("cvI", 448, 512), A("f", 288, 352), 2.0 ** 13, OP.mult)
-        else:
-            tt(A("cvS", 224, 256), A("ps2", 32 * r, 32 * r + 32), thr, OP.subtract)
-            tt(A("cvI", 224, 256), A("ps1", 32 * r, 32 * r + 32), thr, OP.subtract)
-            tree(dS, "cvS", "lS%d" % t, 32)
-            tt(sc, A("KP"), A("ps0", 32, 64), OP.add)
-            ts(pay, dS, 0.0, OP.is_lt, 8192.0, OP.mult)
-            ts(dS, dS, 2.0 ** 26, OP.mult)
-            tt(pay, pay, sc, OP.add)
-        tt(A("UX"), I(A("I16"), sl), A("G"), OP.mult)
-        conv(A("ps4", 64, 80), "ZA", lambda b: A("UX", 16 * b, 16 * b + 16))
-        if r == t:
-            conv(A("ps4", 16, 32), "ZA", lambda a: A("UX", a, L, 16))
+        act(A("UB", 1280, V), I(A("W1"), A(P, 80, 128)))
+        tt(A("cvI", 448, 512, 2), A("ps2", 32 * r, 32 * r + 32), thr, OP.subtract)
+        tt(A("cvI", 449, 512, 2), A("ps1", 32 * r, 32 * r + 32), thr, OP.subtract)
         for b in range(2):
-            mm(A("ps%d" % (1 + b)), A("ID"), A("X", 512 + 512 * b, 1024 + 512 * b), True, True)
+            mm(A("ps%d" % (1 + b)), A("ID"), A("X", 1024 + 512 * b, 1536 + 512 * b), True, True)
+        if not t:
+            ts(A("ZY"), A("i1"), c15, OP.is_equal, row7, OP.mult)
+        conv(A("ps5", 0, 80), "ZY", lambda a: A("UB", a, 1280, 16))
+        conv(A("ps5", 80, 144), "ZY", lambda a: A("UB", 1280 + a, W, 16))
 
-        if MERGE:
-            ts(A("ps6", 0, 256), A("lI%d" % t, 0, 256), 2.0 ** 13, OP.mult)
-            ts(A("cvI", 256, 448), A("lI%d" % t, 256, 448), 2.0 ** 13, OP.mult)
-            tt(A("ps7", 0, 128), A("ps6", 0, 128), A("cvI", 256, 384), OP.add)
-            tt(A("tr", 0, 128), A("ps6", 128, 256), A("cvI", 384, 512), OP.add)
-            tt(A("tr", 128, 256), A("ps7", 0, 128), A("tr", 0, 128), OP.add)
-            tt(A("f", 64, 128), A("tr", 128, 192), A("tr", 192, 256), OP.add)
-            tt(tq, A("f", 64, 128, 2), A("f", 65, 128, 2), OP.mult)
-            ts(pay, A("f", 64, 128, 2), 0.0, OP.is_lt, 8192.0, OP.mult)
-            tt(A("SC", 1, 33), tq, A("ps0", 0, 32), OP.max)
-            tt(pay, pay, sc, OP.add)
-        else:
-            tree(dI, "cvI", "lI%d" % t, 32)
-            tt(dI, dI, dS, OP.mult)
-            tt(A("SC", 1, 33), dI, A("ps0", 0, 32), OP.max)
+        copy(A("ps6", 0, 256), A("lI%d" % t, 0, 256))
+        copy(A("cvI", 256, 448), A("lI%d" % t, 256, 448))
+        tt(A("ps7", 0, 128), A("ps6", 0, 128), A("cvI", 256, 384), OP.add)
+        tt(A("tr", 0, 128), A("ps6", 128, 256), A("cvI", 384, 512), OP.add)
+        tt(A("tr", 128, 256), A("ps7", 0, 128), A("tr", 0, 128), OP.add)
+        tt(A("f", 64, 128), A("tr", 128, 192), A("tr", 192, 256), OP.add)
+        tt(tq, A("f", 64, 128, 2), A("f", 65, 128, 2), OP.mult)
+        ts(pay, A("f", 64, 128, 2), 0.0, OP.is_lt, 8192.0, OP.mult)
+        tt(A("SC", 1, 33), tq, A("ps0", 0, 32), OP.max)
+        tt(pay, pay, A("ps0", 32, 64), OP.add)
         for a in range(2):
             red(mcol(a), A("SC", 17 * a, 17 * a + 17), OP.min)
         for a in range(2):
@@ -452,16 +435,15 @@ def rank_program(g, core, T, topo):
         place = A("lB%d" % t, 2 * r, 2 * r + 2)
         share("aB%d" % t, msg, lambda d: place, lB[1], place)
 
-        thJ = A("h", 0, 32)
-        okN, e1, e2, val, base, ya, dl, dU, dC = [A("h", 32 + 16 * i, 48 + 16 * i) for i in range(9)]
+        okN, e1, e2, val, base, ya, dl, dU, dC, e3 = [A("h", 32 + 16 * i, 48 + 16 * i) for i in range(10)]
         Po = A("PF", 16 * r, 16 * r + 16)
-        copy(upu, A("ps4", 64, 80))
-        if not t:
-            last_constants()
-        conv(A("ps5", 0, 144), "ZY", lambda a: A("UB", a, W, 16))
-        act(A("XS"), I(A("X"), upu))
-        ts(okN, A("lF%d" % t), float(V), OP.is_lt)
+        copy(A("G"), I(A("PF"), sh))
+        tt(A("UX"), I(A("I16"), sl), A("G"), OP.mult)
+        conv(A("ps4", 64, 80), "ZA", lambda b: A("UX", 16 * b, 16 * b + 16))
         if r == t:
+            conv(A("ps4", 16, 32), "ZA", lambda a: A("UX", a, L, 16))
+        if r == t:
+            ts(okN, A("lF%d" % t), float(V), OP.is_lt)
             tt(e2, ZS, okN, OP.mult)
             ts(A("UU", 0, 128), A("ps5", 0, 128), 15.0, OP.add)
             ts(A("UU", 128, 144), e2, 15.0, OP.add)
@@ -469,79 +451,91 @@ def rank_program(g, core, T, topo):
         else:
             ts(A("UU"), A("ps5", 0, 144), 15.0, OP.add)
             ts(n3, A("ps5", 128, 144), 15.0, OP.add)
+        copy(upu, A("ps4", 64, 80))
+        act(A("XS"), I(A("X"), upu))
         mm(A("ps6", 256, 512), A("ID"), A("XS"), True, True)
-        mm(A("ps0"), A("ID"), A("X", 1536, 2048), True, True)
         conv(A("ps4", 0, 16), "ZL", lambda a: A("UB", L * r + a, L * r + L, 16))
         if r != t:
             conv(A("ps4", 16, 32), "ZL", lambda a: A("UB", V + a, W, 16))
-        act(A("MK"), I(A("IZ"), A("UU", 128, 144)))
-        ts(n4, n3, 4, OP.arith_shift_right)
-        copy(ao, n4)
 
         ts(n0, lB, 8191, OP.bitwise_and)
         ts(n1, lB, 13, OP.arith_shift_right, 1025, OP.bitwise_and)
         copy(cu, n0)
+        copy(fo, n1)
         copy(A("KC", 16, 272), I(A("K"), cu))
-        for b in range(3):
-            act(A("KA", 512 * b, 512 * b + 512), I(A("KC"), A("UU", 32 + 32 * b, 64 + 32 * b)))
+        act(A("MB", 16, 272), I(A("META"), cu))
+        mine_u = A("UU", 16 * r, 16 * r + 16)
+        for b in range(2):
+            act(A("KA", 512 * b, 512 * b + 512), I(A("KC"), A("UU", 64 + 32 * b, 96 + 32 * b)))
+        act(e1, A("ps4", 0, 16), AF.Identity, bias=float(L * t - 1))
+        act(e3, A("ps4", 16, 32), AF.Identity, bias=0.0 if r == t else float(L * t - 1))
         tt(A("PU"), A("KC", 16, 272), A("ps6", 256, 512), OP.mult)
         conv(A("ps6", 0, 16), "ZA", lambda b: A("PU", b, L, 16))
-        tt(A("PC", 0, 512), I(A("KC"), A("UU", 0, 32)), A("X", 0, 512), OP.mult)
-        ts(A("sU%d" % t), A("ps6", 0, 16), BIAS, OP.add)
-        share("aU%d" % t, A("sU%d" % t), lambda d: A("lU%d" % t, 16 * slot(d), 16 * slot(d) + 16), A("lU%d" % t)[1])
-        copy(fo, n1)
-        for b in range(3):
-            tt(A("PC", 512 + 512 * b, 1024 + 512 * b), A("KA", 512 * b, 512 * b + 512), A(("ps1", "ps2", "ps0")[b]), OP.mult)
-            if not b:
-                conv(A("ps7", 0, 64), "ZA", lambda a: A("PC", a, 1024, 16))
-        conv(A("ps7", 64, 128), "ZA", lambda a: A("PC", 1024 + a, V, 16))
-        mine_u = A("UU", 16 * r, 16 * r + 16)
-        act(A("MB", 16, 272), I(A("META"), cu))
+        conv(A("ps3", 0, 16), "ZT", lambda b: A("MB", 16 + b, 272, 16))
         act(A("SB", 16, 272), I(A("SW", 0, 1040), fo))
+        act(A("h", 0, 16), A("ps3", 0, 16), AF.Identity, bias=7 * BIAS + 0.5)
         act(A("MB", 272, 528), I(A("MB", 0, 272), mine_u))
         act(A("SB", 272, 528), I(A("SB", 0, 272), mine_u))
-        ts(e1, A("ps4", 0, 16), float(L * t - 1), OP.add)
-        if r == t:
-            tt(val, A("ps4", 16, 32), Po, OP.subtract)
-        else:
-            ts(e2, A("ps4", 16, 32), float(L * t - 1), OP.add)
-        ts(A("sC%d" % t), A("ps7", 0, 128), BIAS, OP.add)
-        deal("aC%d" % t, "sC%d" % t, "lC%d" % t, 16)
-
-        conv(A("ps3", 0, 32), "ZT", lambda a: A("MB", 16 + a, 528, 16))
-        conv(A("ps4", 32, 64), "ZY", lambda a: A("SB", 16 + a, 528, 16))
-        if t + 1 < R:
-            clear_window()
-            expand(t + 1)
+        tt(A("PC", 0, 384), I(A("KC"), A("UU", 0, 24)), A("X", 0, 384), OP.mult)
+        ts(A("sU%d" % t), A("ps6", 0, 16), BIAS, OP.add)
+        share("aU%d" % t, A("sU%d" % t), lambda d: A("lU%d" % t, 16 * slot(d), 16 * slot(d) + 16), A("lU%d" % t)[1])
+        tt(A("PC", 384, 1024), I(A("KC"), A("UU", 24, 64)), A("X", 384, 1024), OP.mult)
+        conv(A("ps7", 0, 64), "ZA", lambda a: A("PC", a, 1024, 16))
+        for b in range(2):
+            tt(A("PC", 1024 + 512 * b, 1536 + 512 * b), A("KA", 512 * b, 512 * b + 512), A("ps%d" % (1 + b)), OP.mult)
+        conv(A("ps7", 64, 128), "ZA", lambda a: A("PC", 1024 + a, V, 16))
+        conv(A("ps5", 256, 272), "ZY", lambda b: A("SB", 16 + b, 272, 16))
+        conv(A("ps0", 0, 16), "ZT", lambda a: A("MB", 272 + a, 528, 16))
+        conv(A("ps4", 48, 64), "ZY", lambda a: A("SB", 272 + a, 528, 16))
+        ts(n4, n3, 4, OP.arith_shift_right)
         tt(dl, e1, Po, OP.subtract)
+        tt(val, e3, Po, OP.subtract)
+        copy(ao, n4)
         if r == t:
             tt(e2, e1, VN, OP.not_equal)
             tt(dl, dl, e2, OP.mult)
-        else:
-            tt(val, e2, Po, OP.subtract)
-        ts(thJ, A("ps3", 0, 32), 7 * BIAS + 0.5, OP.add)
+        ts(A("sC%d" % t), A("ps7", 0, 128), BIAS, OP.add)
+        deal("aC%d" % t, "sC%d" % t, "lC%d" % t, 16)
+
+        act(A("MK"), I(A("IZ"), A("UU", 128, 144)))
+        act(A("h", 16, 32), A("ps0", 0, 16), AF.Identity, bias=7 * BIAS + 0.5)
+        if t + 1 < R:
+            expand(t + 1)
         tt(A("cvU", 112, 128), A("ps6", 0, 16), A("h", 0, 16), OP.subtract)
-        tt(A("cvC", 112, 128), A("ps7", 16 * r, 16 * r + 16), A("h", 16, 32), OP.subtract)
         tree(dU, "cvU", "lU%d" % t, 16)
-        tt(dU, dU, A("ps4", 32, 48), OP.mult)
+        tt(dU, dU, A("ps5", 256, 272), OP.mult)
+        tt(A("cvC", 112, 128), A("ps7", 16 * r, 16 * r + 16), A("h", 16, 32), OP.subtract)
         ts(A("OW", 1, 17), dU, 0.0, OP.is_gt)
         tt(A("OG"), I(A("OW", 0, 17), ao), A("MK"), OP.mult)
         conv(A("ps6", 16, 32), "ZA", lambda a: A("OG", a, L, 16))
-        ts(ya, A("ps6", 16, 32), 0.5, OP.is_lt)
-        tt(base, A("ps6", 16, 32), val, OP.mult)
-        tt(ya, ya, A("ps4", 48, 64), OP.mult)
-        tt(base, base, Po, OP.add)
 
         tree(dC, "cvC", "lC%d" % t, 16)
-        tt(dC, dC, ya, OP.mult)
+        tt(dC, dC, A("ps4", 48, 64), OP.mult)
         ts(dC, dC, 0.0, OP.is_gt)
         tt(dC, dC, dl, OP.mult)
-        tt(dC, dC, base, OP.add)
+        tt(ya, val, dC, OP.subtract)
+        tt(base, dC, Po, OP.add)
+        tt(ya, ya, A("ps6", 16, 32), OP.mult)
+        tt(base, base, ya, OP.add)
         mine = A(Pn, 16 * r, 16 * r + 16)
-        copy(mine, dC)
-        share("aD%d" % t, mine, lambda d: mine, [(Pn, 16 * d, 16 * d + 16) for d in peers])
+        copy(mine, base)
+        lead = t + 1 if t + 1 < R else None
+        share("aS%d" % t if r == lead else "aD%d" % t, mine, lambda d: mine, [])
+        if r == lead:
+            del totals["aS%d" % t]
+        elif lead is not None:
+            landed("aS%d" % t, len(lanes), [(Pn, 16 * lead, 16 * lead + 16)])
+        rest = [d for d in peers if d != lead]
+        landed("aD%d" % t, len(lanes) * len(rest), [(Pn, 16 * d, 16 * d + 16) for d in rest])
+        if t + 1 < R:
+            clear_window()
 
+        if not t:
+            tt(cZ, cW, row7, OP.add)
+            ts(A("ZZ"), A("i1"), c15, OP.is_equal, cZ, OP.mult)
         tt(A("AC"), I(A("SW", 16, 1056), fo), A("MB", 16, 272), OP.mult)
+        if r != t:
+            ts(okN, A("lF%d" % t), float(V), OP.is_lt)
         conv(A("ps3", 64, 80), "ZZ", lambda a: A("AC", 16 * a, 16 * a + 16))
         tt(e1, A("ps3", 64, 80), okN, OP.mult)
         ts(A("YC", 16 * t, 16 * t + 16), e1, -1.0, OP.add)

@@ -5,9 +5,11 @@ N, V, C, L, R = 8, 2048, 6144, 256, 3
 W = V + L
 BIAS = 32768.0
 Q = C // 16
-MERGE = True
+HALVES = "SSSSSVSSSVSSVSSS"
+BULK = ("VSVSVSV", "VSVSVSV", "VSVSVSVS")
 
 SCRATCH = {}
+WIDTH = {"bfloat16": 2, "float16": 2, "uint16": 2, "float32": 4, "int32": 4}
 
 
 def _sb(name, cols, dtype):
@@ -16,535 +18,685 @@ def _sb(name, cols, dtype):
 
 for _n, _c, _d in [
     ("K", C, "bfloat16"), ("X", V, "bfloat16"), ("CD", V, "int32"), ("PA", 128, "int32"), ("META", C, "bfloat16"),
-    ("BC", 2 * Q, "int32"), ("BR", 2 * Q, "float32"), ("CP", 8 * Q, "bfloat16"),
-    ("W1", W, "bfloat16"), ("UB", W, "bfloat16"), ("KG", 4096, "bfloat16"), ("PI", 4096, "float16"), ("PS", 4096, "float16"),
-    ("XE0", 2048, "bfloat16"), ("XE1", 2048, "bfloat16"), ("XE2", 2048, "bfloat16"), ("BA", 2048, "float16"),
-    ("PC", V, "float16"), ("PU", L, "float16"), ("XS", L, "bfloat16"), ("KC", 272, "bfloat16"), ("KA", 1536, "bfloat16"),
-    ("MB", 528, "bfloat16"), ("SB", 528, "bfloat16"), ("MG", 512, "bfloat16"), ("E", L, "uint16"), ("EO", 32, "uint16"),
-    ("i1", 144, "float32"), ("i3", 256, "float32"), ("i4", 256, "float32"), ("i5", 256, "float32"),
-    ("ii", 32, "int32"), ("col", 32, "float32"), ("I16", 16, "float32"),
+    ("BC", 2 * Q, "int32"), ("CP", 6 * Q, "bfloat16"), ("CI", Q, "bfloat16"), ("XB", 16 * L, "bfloat16"),
+    ("XI", R * L, "bfloat16"), ("XO", 16 * R, "uint16"), ("i7", 16 * R, "float32"),
+    ("W1", W, "bfloat16"), ("KW", W, "bfloat16"), ("UB", 2 * L, "bfloat16"), ("UL", 2 * L, "bfloat16"), ("KG", 4096, "bfloat16"), ("BA", 2048, "float16"),
+    ("PC", V, "float16"), ("PX", 3 * L, "float16"), ("XS", L, "bfloat16"), ("XG", L, "bfloat16"), ("XL", 2 * L, "bfloat16"),
+    ("KC", 272, "bfloat16"), ("KA", V, "bfloat16"),
+    ("MS", 1568, "bfloat16"), ("MG", 512, "bfloat16"), ("E", L, "uint16"),
+    ("i1", 144, "float32"), ("i3", 256, "float32"), ("i4", 128, "float32"), ("i5", 256, "float32"), ("i6", 256, "float32"),
+    ("ii", 32, "int32"), ("col", 32, "float32"), ("I16", 16, "float32"), ("G8", 8, "float32"),
     ("ZA", 144, "float16"), ("ZT", 144, "bfloat16"), ("ZW", 144, "bfloat16"), ("ZC", 144, "bfloat16"), ("ZY", 144, "bfloat16"),
-    ("ZZ", 144, "bfloat16"), ("ZL", 144, "bfloat16"), ("ID", 128, "bfloat16"), ("BK", 128, "float16"), ("JJ", L, "float16"),
-    ("IZ", 272, "bfloat16"), ("ZV", L, "bfloat16"), ("SW", 1056, "bfloat16"), ("SC", 34, "float32"), ("ST", 64, "float32"), ("KP", 32, "bfloat16"),
-    ("PF", 128, "float32"), ("SF", 16, "float32"), ("S16", 16, "float16"), ("UX", L, "float16"), ("G", L, "float32"),
-    ("EK", 2 * L, "float32"), ("EK2", 2 * L, "float32"), ("e", 32, "float32"), ("UU", 144, "uint16"),
-    ("cvS", 256, "float32"), ("cvI", 512, "float32"), ("cvU", 128, "float32"), ("cvC", 128, "float32"),
-    ("tr", 384, "float32"), ("f", 384, "float32"), ("h", 256, "float32"), ("n", 128, "int32"), ("u", 128, "uint16"),
-    ("OW", 24, "float32"), ("MK", L, "bfloat16"), ("OG", L, "float16"), ("AC", L, "bfloat16"), ("YC", 48, "float32"),
+    ("ZR", 256, "bfloat16"), ("SZ", 288, "bfloat16"), ("SP", 288, "bfloat16"),
+    ("ID", 128, "bfloat16"), ("BK", 128, "float16"), ("JJ", L, "float16"),
+    ("IZ", 272, "bfloat16"), ("ZV", R * L, "bfloat16"), ("SW", 1040, "bfloat16"), ("ZK", 48, "bfloat16"),
+    ("KP", 32, "bfloat16"), ("A2", 64, "bfloat16"),
+    ("PF", 128, "float32"), ("S16", 16, "float16"), ("UX", L, "float16"), ("G", L, "float32"),
+    ("EK", 2 * L, "float32"), ("UU", 144, "uint16"), ("U2", 32, "uint16"),
+    ("f", 5120, "float32"), ("n", 512, "int32"), ("u", 512, "uint16"),
+    ("OW", 24, "float32"), ("MK", L, "bfloat16"), ("OG", L, "float16"), ("YC", 48, "float32"),
     ("YP", 128, "float32"), ("P0", 128, "uint16"),
 ]:
     _sb(_n, _c, _d)
 for _t in range(R):
-    for _n, _c, _d in [("sS", 256, "uint16"), ("sI", 512 if MERGE else 256, "uint16"), ("lS", 224, "uint16"),
-                       ("lI", 448 if MERGE else 224, "uint16"),
-                       ("sB", 4, "int32"), ("lB", 16, "int32"), ("sU", 16, "uint16"), ("lU", 112, "uint16"),
+    for _n, _c, _d in [("H", 16, "uint16"), ("sI", 896, "uint16"), ("lI", 448, "uint16"), ("sB", 4, "int32"), ("lB", 16, "int32"),
+                       ("sX", 48, "uint16"), ("lU", 112, "uint16"), ("lL", 224, "uint16"),
                        ("sC", 128, "uint16"), ("lC", 112, "uint16"), ("sF", 8, "uint16"), ("lF", 16, "uint16")]:
         _sb("%s%d" % (_n, _t), _c, _d)
     _sb("P%d" % (_t + 1), 128, "uint16")
 for _b in range(8):
     SCRATCH["ps%d" % _b] = ("psum", [128, 512], "float32")
 
-SEMAPHORES = (["qV", "qS", "qP", "qG", "sent"] + ["d%d" % i for i in range(16)]
-              + ["%s%d" % (x, t) for x in ("aF", "aS", "aI", "aB", "aU", "aC", "aD") for t in range(R)])
+SEMAPHORES = (["qV", "qS", "qP", "qG", "sent"] + ["d%d" % i for i in range(24)]
+              + ["%s%d" % (x, t) for x in ("aF", "aS", "aB", "aU", "aL", "aC", "aD", "aI0", "aI1", "aI2", "aI3") for t in range(R)])
+
+CYCLE, PE, GATHER, SCATTER, SIGNAL, START, ROW, BYTE, ISSUE = 0.83e-3, 0.42e-3, 1.56, 3.8, 0.05, 0.8, 0.012, 1 / 25e3, 0.3
+PLAN = {}
+
+
+def A(name, lo=0, hi=None, step=1, rows=(0, 128)):
+    if hi is None:
+        hi = SCRATCH[name][1][1]
+    return ((name, (slice(*rows), slice(lo, hi, step))), [(name, lo, hi)], -(-(hi - lo) // step))
+
+
+def I(win, off):
+    return ((win[0], off[0], "indirect"), win[1] + off[1], 16 * off[2])
+
+
+def hbm(name, *index):
+    return ((name, index or (slice(None),)), [], 0)
+
+
+def sl16(name, d, n=1):
+    return A(name, 16 * d, 16 * (d + n))
+
+
+def describe(r, cores, topo, steps, arrivals):
+    hist, used, totals = {}, {"f": 0, "n": 0, "u": 0, "d": 0}, {"sent": 0}
+
+    def step(q, calls, time, reads, writes, sem=None, rows=None, after=()):
+        me = len(steps)
+        hard, soft, banks = set(after), set(), set()
+        for (name, lo, hi), wr in [(k, False) for k in reads] + [(k, True) for k in writes]:
+            seen = hist.setdefault(name, [])
+            if name.startswith("ps"):
+                banks.add(name)
+            for l2, h2, w2, q2, i in seen:
+                if q == q2 == "P":
+                    if name in banks:
+                        soft.add(i)
+                elif l2 < hi and lo < h2 and (wr or w2):
+                    hard.add(i)
+            if wr:
+                seen[:] = [x for x in seen if not (lo <= x[0] and x[1] <= hi) or x[4] == me]
+            seen.append((lo, hi, wr, q, me))
+        hard.discard(me)
+        soft.discard(me)
+        steps.append({"rank": r, "q": q, "calls": calls, "time": time, "hard": hard, "soft": soft, "banks": banks, "sem": sem,
+                      "rows": rows})
+        return me
+
+    def new(pool, cols=16):
+        used[pool] += -(-cols // 8) * 8
+        return A(pool, used[pool] - -(-cols // 8) * 8, used[pool] - -(-cols // 8) * 8 + cols)
+
+    def cut(a, lo, hi, by=1):
+        name, base, _ = a[1][0]
+        return A(name, base + lo, base + hi, by)
+
+    def laced(name, lo, b):
+        return (A(name, lo + b, lo + 2 * L, 2)[0], [(name, lo + L * b, lo + L * b + L)], L)
+
+    def both(name, base, lo, hi, by=1):
+        a = A(name, base + lo, base + hi, by)
+        return (a[0], [(name, base, base + 2 * L)], a[2])
+
+    def keys(ins):
+        return [k for a in ins if isinstance(a, tuple) for k in a[1]]
+
+    def op(q, name, args, cycles, kw=None):
+        out, ins = args[0], list(args[1:]) + list((kw or {}).values())
+        if len(out[0]) == 3:
+            time = 0.05 + out[2] * SCATTER * CYCLE
+        elif isinstance(args[1], tuple) and len(args[1][0]) == 3:
+            time = 0.06 + out[2] * GATHER * CYCLE
+        else:
+            time = (0.03 if q == "V" else 0.06) + max(64, cycles) * CYCLE
+        step(q, [(name, args, kw or {})], time, keys(ins) + out[1][1:], out[1][:1])
+
+    def short(*ops):
+        return 0.5 if all(WIDTH[SCRATCH[a[1][0][0]][2]] == 2 for a in ops) else 1
+
+    def copy(out, a):
+        op("V", "tensor_copy", (out, a), out[2] * short(out, a))
+
+    def tt(out, a, b, o):
+        op("V", "tensor_tensor", (out, a, b, o), out[2] * (1 if "ps" in (a[1][0][0][:2], b[1][0][0][:2]) else 2))
+
+    def ts(out, a, s1, o0, s2=None, o1=None):
+        op("V", "tensor_scalar", (out, a, s1, s2, o0) + ((o1,) if o1 else ()), out[2] * short(out, a))
+
+    def red(out, a, o, absolute=False):
+        op("V", "tensor_reduce", (out, a, AxisListType.X, o), a[2], {"apply_absolute_value": absolute})
+
+    def fill(out, v):
+        op("V", "memset", (out, v), out[2] * short(out))
+
+    def act(out, a, fn=AF.Copy, **kw):
+        op("S", "activation", (out, a, fn), out[2], kw)
+
+    def mms(group):
+        step("P", [("matmul", m, {}) for m in group], sum(0.013 + max(min(64, m[1][2]), m[2][2]) * PE for m in group),
+             [k for m in group for k in m[1][1] + m[2][1]], [k for m in group for k in m[0][1]])
+
+    def iota(out, pattern, base, mult):
+        kw = {} if SCRATCH[out[1][0][0]][2] == "int32" else {"allow_small_or_imprecise_dtypes": True}
+        step("G", [("iota", (out, pattern, base, mult), kw)], 0.13 + 2 * out[2] * CYCLE, [], out[1])
+
+    def dmas(q, pairs, rows, size, sem=None, reads=(), after=()):
+        if sem is None:
+            used["d"] += 1
+            sem = ("d%d" % (used["d"] - 1), 16 * len(pairs))
+            totals[sem[0]] = sem[1]
+        return step(q, [("dma_start", p, {}) for p in pairs], 0.05 * len(pairs), keys([p[1] for p in pairs]) + list(reads),
+                    keys([p[0] for p in pairs]), sem, (rows, size), after)
+
+    def conv(out, z, src, start=True, stop=True):
+        mms([(out, A(z, 15 - i, 143 - i), src(i), start and i == 0, stop and i == 15) for i in range(16)])
+
+    core = cores[r]
+    peers = [(r + i) % N for i in range(1, N)]
+    lanes = topo.engines(core, cores[peers[0]])
+
+    def slot(d):
+        return (d - r - 1) % N
+
+    def send(sem, transfers):
+        src = transfers[0][1][0]
+        size = src[2] * WIDTH[SCRATCH[src[1][0][0]][2]]
+        rows = max(128 * len(x[2]) * len(lanes) // len(x[0]) for x in transfers)
+        me = step("G", [("remote", sem, transfers)], ISSUE, keys([a for x in transfers for a in x[1]]), [], ("sent", 0), (rows, size))
+        for engines, _, places in transfers:
+            totals["sent"] += len(engines)
+            for d, _ in places:
+                arrivals.setdefault((d, sem), []).append((me, len(engines)))
+
+    def landed(sem, where, own=None):
+        me = step("", [], 0.0, [], where[1] if isinstance(where, tuple) else where, (sem, None))
+        if own is not None:
+            arrivals.setdefault((r, sem), []).append((own, 16))
+        arrivals[(r, sem, "step")] = me
+
+    def deal(sem, dests, src, land):
+        far = [d for d in dests if topo.die(cores[d]) != topo.die(core)]
+        near = [d for d in dests if d not in far]
+        w = len(lanes) >> (len(dests) - 1).bit_length()
+        pool = lanes[0::2] + lanes[:0:-2]
+        send(sem, [(side[w * i:w * i + w], src(d), [(d, land(d))]) for group, side in ((far, pool), (near, pool[::-1]))
+                   for i, d in enumerate(group)])
+
+    def share(sem, src, land, dests=peers):
+        send(sem, [(lanes, [src], [(d, land(d)) for d in dests])])
+
+    def share_list(sem, src, name):
+        place = A(name, 2 * r, 2 * r + 2)
+        share(sem, src, lambda d: place)
+        landed(sem, A(name), dmas("Y", [((place[0], [], 2), src)], 128, 8, (sem, None)))
+
+    def tree(own, land, w):
+        cv, tr, out = new("f", 8 * w), new("f", 6 * w), new("f", w)
+        own(cut(cv, 7 * w, 8 * w))
+        copy(cut(cv, 0, 7 * w), A(land))
+        tt(cut(tr, 0, 4 * w), cut(cv, 0, 4 * w), cut(cv, 4 * w, 8 * w), OP.add)
+        tt(cut(tr, 4 * w, 6 * w), cut(tr, 0, 2 * w), cut(tr, 2 * w, 4 * w), OP.add)
+        tt(out, cut(tr, 4 * w, 5 * w), cut(tr, 5 * w, 6 * w), OP.add)
+        return out
+
+    last = []
+    for name, src, size in (("PA", "pa", 512), ("CD", "cd", 4 * V), ("X", "xv", 2 * V), ("K", "kc", 2 * C)):
+        last = [dmas("Y", [(A(name), hbm(src))], 128, size, after=last and [])]
+    dmas("S", [(A("BC", 0, Q), hbm("bt"))], 128, 4 * Q)
+    dmas("S", [(A("BC", Q, 2 * Q), hbm("co"))], 128, 4 * Q)
+
+    cA, cG, cQ, c8, cJ, cH, c15, cT, cW, cC, cV, cS, cS2, cY, cP, cG2 = [A("col", i, i + 1) for i in range(16)]
+    half, bias, minus, pays = [A("col", 16 + 2 * i, 18 + 2 * i) for i in range(4)]
+    row6, row7, row8 = A("I16", 6, 7), A("I16", 7, 8), A("I16", 8, 9)
+    LN, SPARE, VN, VA, ZS, VO, CB = new("f", 2), new("f", 2), new("f"), new("f"), new("f"), new("f"), new("f")
+    iota(A("ii", 0, 1), [[0, 1]], 0, 1)
+    iota(A("i3"), [[0, 16], [1, 16]], 0, 0)
+    iota(A("i4"), [[1, 8], [0, 16]], 0, 0)
+    iota(A("i5"), [[1, 256]], 0, 0)
+    iota(A("i1"), [[1, 144]], 0, -1)
+    iota(A("CI"), [[1, Q]], -Q // 2, 0)
+    iota(A("i6"), [[100, 8], [0, 2], [1, 16]], -400, 0)
+    iota(A("i7"), [[L, R], [16, 2], [32, N]], 0, 0)
+    iota(A("KP"), [[16384, 16], [0, 2]], 0, 0)
+    for name in ("IZ", "KC", "MS", "OW"):
+        iota(A(name, 0, 16), [[0, 16]], 0, 0)
+    iota(A("MS", 528, 800), [[0, 272]], 0, 0)
+    for i in range(2):
+        fill(A("XB", 4 * L * i, 4 * L * i + 4 * L), 0.0)
+    for i in range(3):
+        iota(A("W1", W // 3 * i, W // 3 * i + W // 3), [[0, W // 3]], 0, 0)
+        fill(A("KW", W // 3 * i, W // 3 * i + W // 3), 0.0)
+    fill(A("SW", 2, 1040), 0.0)
+    for i, (shift, mask) in enumerate(((0, 15), (4, 7), (5, 3), (1, 7), (0, 1), (4, 1))):
+        ts(A("ii", 1 + i, 2 + i), A("ii", 0, 1), shift, OP.arith_shift_right, mask, OP.bitwise_and)
+    copy(A("col", 0, 6), A("ii", 1, 7))
+    ts(A("I16"), A("i3", 0, 16), cA, OP.is_equal)
+    for i in range(2):
+        ts(A("SW", i, i + 1), A("I16", 0, 1), 2.0 * i - 1.0, OP.mult)
+    ts(A("XO"), A("i7"), cA, OP.add)
+    ts(half, A("i5", 0, 2), cJ, OP.is_equal)
+    ts(bias, half, BIAS, OP.mult)
+    ts(minus, half, -1.0, OP.mult)
+    ts(A("BK"), A("i4"), cG, OP.is_equal)
+    ts(A("JJ"), A("i5"), A("I16", 0, 1), OP.mult, 1.0 / 512, OP.mult)
+    for a in range(16):
+        ts(A("BA", 128 * a, 128 * a + 128), A("BK"), A("I16", a, a + 1), OP.mult)
+    ts(c15, cA, -1.0, OP.mult, 15.0, OP.add)
+    ts(VN, A("i5", 0, 256, 16), cA, OP.add)
+    ts(LN, cut(VN, 2 * r, 2 * r + 2), 1.0 / 512, OP.mult)
+    ts(SPARE, cut(VN, 2 * r, 2 * r + 2), float(V), OP.add)
+    ts(A("G8"), A("i5", 0, 8), cG, OP.is_equal)
+    red(cT, A("I16", 0, 3), OP.add)
+    red(cW, A("I16", 3, 6), OP.add)
+    tt(cC, row8, row6, OP.add)
+    tt(cY, row6, row7, OP.add)
+    ts(cV, cW, 2.0 ** -23, OP.mult)
+    ts(cS, c8, 16.0, OP.mult, 3.0, OP.add)
+    ts(cS2, cQ, 4.0, OP.mult, cS, OP.add)
+    ts(cP, cH, -8192.0, OP.mult, 8192.0, OP.add)
+    ts(pays, half, cP, OP.mult)
+    ts(cG2, cG, 2.0, OP.mult)
+    ts(A("ZA"), A("i1"), c15, OP.is_equal)
+    ts(A("ID"), A("i1", 0, 128), 0.0, OP.is_equal)
+    for name, weight in (("ZY", cY), ("ZW", cV), ("ZC", cC), ("ZT", cT)):
+        ts(A(name), A("i1"), c15, OP.is_equal, weight, OP.mult)
+    ts(A("ZR"), A("i6"), cG2, OP.is_equal, cT, OP.mult)
+    for b in range(2):
+        ts(A("SZ", 144 * b, 144 * b + 144), A("i5", 0, 144), cS2, OP.is_equal, cut(half, b, b + 1), OP.mult)
+        ts(A("SP", 144 * b, 144 * b + 144), A("i5", 0, 144), cS2, OP.is_equal, cut(pays, b, b + 1), OP.mult)
+    fill(A("ZK", 0, 2), 0.5)
+    fill(A("ZK", 2, 34), -1.0)
+    ts(A("ZV", 0, L), A("i5"), 1.0, OP.add, row7, OP.mult)
+    for i in range(1, R):
+        z = new("f", 1)
+        act(z, row6, AF.Identity, scale=float(L * i))
+        act(A("ZV", L * i, L * i + L), A("ZV", 0, L), AF.Identity, bias=z)
+    act(A("EK", 0, L), A("i3"), AF.Abs, bias=cA, scale=-1.0)
+    act(A("IZ", 16, 272), A("EK", 0, L), AF.Relu, bias=1.0, scale=-1.0)
+    if r < R:
+        act(ZS, VN, AF.Identity, bias=1.0)
+        act(VO, VN, AF.Identity, bias=float(L * r + 4096))
+    copy(A("P0"), A("PA"))
+    for b in range(2):
+        copy(A("H0", 8 * b, 8 * b + 8), A("PA", b, 16, 2))
+
+    ts(VA, A("i3", 0, 16), float(Q), OP.mult, Q / 2, OP.add)
+    ts(CB, VA, row8, OP.mult)
+    for i in range(16):
+        act(A("META", Q * i, Q * i + Q), A("CI"), AF.Identity, bias=cut(CB, i, i + 1), scale=row6)
+    for i in range(2):
+        rest = A("ps%d" % (1 + i), 0, Q)
+        copy(A("CP", i * Q, i * Q + Q), A("BC", i * Q, i * Q + Q))
+        tt(rest, A("BC", i * Q, i * Q + Q), A("CP", i * Q, i * Q + Q), OP.subtract)
+        act(A("CP", (2 + i) * Q, (3 + i) * Q), rest)
+        tt(A("CP", (4 + i) * Q, (5 + i) * Q), rest, A("CP", (2 + i) * Q, (3 + i) * Q), OP.subtract)
+    dmas("Y", [((("META", (slice(row, 128, 16), slice(None))), A("META")[1], 0), A("CP", part * Q, part * Q + Q))
+               for row, part in enumerate((0, 2, 4, 1, 3, 5))], 6 * 128, 2 * Q, reads=A("K")[1])
+
+    for t in range(R):
+        P, Pn = "P%d" % t, "P%d" % (t + 1)
+        lead = t + 1 if t + 1 < R else None
+        s = sl16(P, t)
+        sI, lI, lB, lF, sX = "sI%d" % t, "lI%d" % t, A("lB%d" % t), A("lF%d" % t), "sX%d" % t
+
+        def slot_list(out, src):
+            ts(out, src, float(L * t), OP.max, float(15 - L * t), OP.add)
+
+        act(A("XI", L * t, L * t + L), I(A("X"), sl16("XO", t)))
+        dmas("Y", [(A("XB", b * L, b * L + L, rows=(16 * b, 16 * b + 16)), A("XI", L * t, L * t + L, rows=(16 * b, 16 * b + 16)))
+                   for b in range(8)], 128, 2 * L)
+        copy(A("E"), I(A("CD"), A("H%d" % t)))
+        act(A("XS"), I(A("X"), A("H%d" % t)))
+        for b in range(8):
+            ts(A("XB", (8 + b) * L, (9 + b) * L), A("XS"), A("G8", b, b + 1), OP.mult)
+        if t:
+            for b in range(2):
+                copy(A(P, 16 * t + b, 16 * t + 16, 2), A("H%d" % t, 8 * b, 8 * b + 8))
+
+        sf, neg, off, inside, low, aim, gap, no = [new("f", 2) for _ in range(8)]
+        copy(A("S16"), s)
+        copy(sf, cut(s, 2 * r, 2 * r + 2))
+        mms([(A("ps4", 0, 256), A("BK"), A("JJ"), True, False)]
+            + [(A("ps4", a, 256, 16), A("BA", 128 * a, 128 * a + 128), A("S16"), False, a == 15) for a in range(16)])
+        act(neg, sf, AF.Identity, scale=-1.0)
+        act(off, sf, AF.Abs, bias=-(L * t + 127.5))
+        act(inside, off, AF.Relu, bias=128.0, scale=-1.0)
+        tt(aim, inside, LN, OP.add)
+        tt(gap, SPARE, sf, OP.subtract)
+        for b in range(2):
+            act(A("EK", L * b, L * b + L), A("ps4", 0, 256), AF.Abs, bias=cut(neg, b, b + 1))
+            red(cut(low, b, b + 1), A("EK", L * b, L * b + L), OP.min)
+            ts(cut(no, b, b + 1), cut(low, b, b + 1), cut(aim, b, b + 1), OP.not_equal, cut(gap, b, b + 1), OP.mult)
+            ts(A("sF%d" % t, b, b + 1), cut(no, b, b + 1), cut(sf, b, b + 1), OP.add)
+        share_list("aF%d" % t, A("sF%d" % t, 0, 2), "lF%d" % t)
+
+        for i, d in enumerate(peers + [r]):
+            bank, c0 = ("ps%d" % (i // 2 % 2), 128 * (i % 2)) if d != r else ("ps2", 0)
+            for b in range(2):
+                (copy if HALVES[2 * i + b] == "V" else act)(laced("KG", 2 * L * d, b), I(A("K"), sl16("E", 8 * b + d)))
+            for h in range(2):
+                mms([(A(bank, c0 + 32 * (a % 4), c0 + 32 * (a % 4) + 32, rows=(32 * (a // 4), 32 * (a // 4) + 32)),
+                      A("XB", 16 * d + a, 16 * L, 128), both("KG", 2 * L * d, 32 * a, 32 * a + 32), True, True)
+                     for a in range(8 * h, 8 * h + 8)])
+            if d != r and (i % 2 or i == N - 2):
+                j = i // 2
+                lo, hi = 128 * j, 64 * i + 64
+                for b in range(2):
+                    ts(A(sI, 448 * b + lo, 448 * b + hi), A(bank, b, c0 + 128, 2), cut(half, b, b + 1), OP.mult,
+                       cut(bias, b, b + 1), OP.add)
+                deal("aI%d%d" % (j, t), peers[2 * j:2 * j + 2],
+                     lambda d: [A(sI, 448 * b + 64 * slot(d), 448 * b + 64 * slot(d) + 64) for b in range(2)],
+                     lambda d: A(lI, 64 * slot(d), 64 * slot(d) + 64))
+                landed("aI%d%d" % (j, t), A(lI, lo, hi))
+
+        for b in range(2):
+            act(laced("MG", 0, b), I(A("META"), sl16("E", 8 * b + r)))
+        mms([(A("ps3", 0, 64), A("ZR", 128 - 32 * (o // 2) - o % 2, 256 - 32 * (o // 2) - o % 2),
+              both("MG", 0, 128 * (o // 2) + o % 2, 128 * (o // 2) + 128, 2), o == 0, o == 7) for o in range(8)])
+        z, pay = A("ps5", 2, 34), A("ps6", 0, 32)
+        mms([(A("ps5", 0, 34), A("ID"), A("ZK", 0, 34), True, False)])
+        conv(z, "ZW", lambda a: both("MG", 0, 32 * a, 32 * a + 32), False, False)
+        mms([(pay, A("ID"), A("KP"), True, False)])
+        conv(pay, "ZC", lambda a: both("MG", 0, 32 * a, 32 * a + 32), False, False)
+        thr, a0_, a1_, a2_, y0, y1 = new("f", 64), new("f", 64), new("f", 64), new("f", 64), new("f", 128), new("f", 128)
+        own = new("f", 128)
+        for b in range(2):
+            act(cut(own, 64 * b, 64 * b + 64), A("ps2", b, 128, 2), AF.Identity, scale=cut(minus, b, b + 1),
+                bias=(1 - b) * (7 * BIAS + 0.5))
+        tt(thr, cut(own, 0, 64), A("ps3", 0, 64), OP.add)
+        tt(a0_, thr, cut(own, 64, 128), OP.add)
+        copy(y0, A(lI, 0, 128))
+        copy(A("ps2", 128, 256), A(lI, 128, 256))
+        tt(y1, A("ps2", 128, 256), y0, OP.add)
+        copy(A("ps2", 256, 384), A(lI, 256, 384))
+        tt(A("ps2", 128, 256), A("ps2", 256, 384), y1, OP.add)
+        tt(a1_, a0_, A("ps2", 128, 192), OP.subtract)
+        tt(a2_, a1_, A("ps2", 192, 256), OP.subtract)
+
+        copy(A("ps2", 448, 512), A(lI, 384, 448))
+        tt(A("A2"), A("ps2", 448, 512), a2_, OP.is_gt)
+        for name, out in (("SZ", z), ("SP", pay)):
+            mms([(cut(out, b, 32, 2), A(name, 144 * b + 3 - h, 144 * b + 131 - h), sl16("A2", h), False, b == 1 and h == 3)
+                 for b in range(2) for h in range(4)])
+        least, over, key = new("f", 2), new("f", 32), new("f", 32)
+        for b in range(2):
+            red(cut(least, b, b + 1), A("ps5", b, 34, 2), OP.min, True)
+            ts(cut(over, b, 32, 2), cut(z, b, 32, 2), cut(least, b, b + 1), OP.not_equal, 2.0 ** 23, OP.mult)
+        tt(key, over, pay, OP.add)
+        for b in range(2):
+            red(A("sB%d" % t, b, b + 1), cut(key, b, 32, 2), OP.min)
+        share_list("aB%d" % t, A("sB%d" % t, 0, 2), "lB%d" % t)
+
+        cand, okN, e3 = new("f", 32), new("f"), new("f")
+        copy(I(A("W1"), lF), A("ZV", L * t, L * t + L))
+        ts(okN, lF, float(V), OP.is_lt)
+        if lead is not None:
+            act(A("UL", 0, L), I(A("W1"), sl16(P, lead)))
+            act(A("UL", L, 2 * L), A("W1", L * lead, L * lead + L))
+            conv(A("ps7", 288, 320), "ZY", lambda a: A("UL", a, 2 * L, 16))
+            slot_list(A("U2"), A("ps7", 288, 320))
+            if r == lead:
+                act(cut(cand, 0, 16), A("ps7", 288, 304), AF.Identity, bias=4095.0)
+                act(cut(cand, 16, 32), A("ps7", 304, 320), AF.Identity, bias=8191.0)
+            dmas("Y", [(A("XL", 0, L), hbm("xv", slice(None), slice(L * lead, L * lead + L)))], 128, 2 * L)
+            act(A("XL", L, 2 * L), I(A("X"), sl16(P, lead)))
+        order_c = [d for d in peers + [r] if d != lead]
+        nc = len(order_c)
+        chunks = [(0, nc)] if lead is not None else [(0, 4), (4, 7), (7, 8)]
+        below = r != t
+        if r != lead:
+            act(A("UB", 0, L), I(A("W1"), sl16(P, r)))
+            if below:
+                act(A("UB", L, 2 * L), A("W1", L * r, L * r + L))
+            conv(sl16("ps7", 0, 1 + below), "ZY", lambda a: A("UB", a, L + L * below, 16))
+            slot_list(sl16("UU", 0, 1 + below), sl16("ps7", 0, 1 + below))
+            act(cut(cand, 0, 16), sl16("ps7", 0), AF.Identity, bias=4095.0)
+
+        n0, n1, n2, sh, sl, upu = new("n"), new("n"), new("n"), new("u"), new("u"), new("u")
+        copy(n0, s)
+        copy(A("PF"), A(P))
+        ts(n1, n0, 4, OP.arith_shift_right)
+        ts(n2, n0, 15, OP.bitwise_and)
+        copy(sh, n1)
+        copy(sl, n2)
+        act(A("G"), I(A("PF"), sh))
+        tt(A("UX"), I(A("I16"), sl), A("G"), OP.mult)
+        conv(A("ps4", 320, 336), "ZA", lambda a: A("UX", a, L, 16))
+        copy(upu, A("ps4", 320, 336))
+        act(A("XG"), I(A("X"), upu))
+
+        if r != lead:
+            n3, n4, ao, e2 = new("n"), new("n"), new("u"), new("f")
+            if r == t:
+                act(e3, A("ps4", 320, 336), AF.Identity, bias=8192.0)
+                tt(e2, ZS, okN, OP.mult)
+                ts(sl16("UU", 1), e2, 15.0, OP.add)
+                ts(n3, e2, 15.0, OP.add)
+                tt(e2, cut(cand, 0, 16), VO, OP.not_equal)
+                tt(cut(cand, 0, 16), cut(cand, 0, 16), e2, OP.mult)
+            else:
+                slot_list(n3, sl16("ps7", 1))
+                act(e3, sl16("ps7", 1), AF.Identity, bias=8191.0)
+            ts(n4, n3, 4, OP.arith_shift_right)
+            copy(ao, n4)
+            act(A("MK"), I(A("IZ"), sl16("UU", 1)))
+
+        m0, m1, cu, fo = new("n"), new("n"), new("u"), new("u")
+        ts(m0, lB, 8191, OP.bitwise_and)
+        copy(cu, m0)
+        act(A("KC", 16, 272), I(A("K"), cu))
+        tt(A("PX", 0, L), I(A("K"), cu), A("XG"), OP.mult)
+        nx = 48 if lead is not None else 16
+        if lead is not None:
+            tt(A("PX", L, 3 * L), I(A("KC"), A("U2")), A("XL"), OP.mult)
+        conv(A("ps6", 64, 64 + nx), "ZA", lambda a: A("PX", a, 16 * nx, 16))
+        ts(A(sX, 0, nx), A("ps6", 64, 64 + nx), BIAS, OP.add)
+        if lead is not None and r != lead:
+            share("aL%d" % t, A(sX, 16, 48), lambda d: A("lL%d" % t, 32 * slot(d), 32 * slot(d) + 32), [lead])
+        share("aU%d" % t, A(sX, 0, 16), lambda d: sl16("lU%d" % t, slot(d)), [d for d in peers if d != lead])
+
+        nm = 48 if r == lead else 32
+        mine_u = A("U2") if r == lead else sl16("UU", 0)
+        sign = A("ps3", 113, 161)
+        hT, c1, c2, c3, a1 = new("f", 48), new("f"), new("f"), new("f"), new("f")
+        ts(m1, lB, 13, OP.arith_shift_right, 1025, OP.bitwise_and)
+        copy(fo, m1)
+        act(A("MS", 16, 272), I(A("META"), cu))
+        act(A("MS", 272, 16 + 16 * nm), I(A("MS", 0, 272), mine_u))
+        act(A("MS", 800, 1056), I(A("SW"), fo))
+        act(A("MS", 1056, 800 + 16 * nm), I(A("MS", 784, 1056), mine_u))
+        conv(A("ps3", 64, 113 + nm), "ZT", lambda a: A("MS", 16 + a, 800 + 16 * nm, 16))
+        act(cut(hT, 0, nm), A("ps3", 64, 64 + nm), AF.Identity, bias=7 * BIAS + 0.5)
+        conv(A("ps4", 256, 272), "ZW", lambda a: A("MS", 16 + a, 272, 16))
+        act(c1, A("ps4", 256, 272), AF.Identity, bias=1.0, scale=2.0 ** 23)
+        act(a1, cut(sign, 0, 16), AF.Abs)
+        tt(c2, c1, okN, OP.mult)
+        tt(c3, c2, a1, OP.mult)
+        act(sl16("YC", t), c3, AF.Identity, bias=-1.0)
+
+        copy(I(A("KW"), lF), A("KC", 16, 272))
+        by_s = [d for i, d in enumerate(order_c) if BULK[t][i] == "S"]
+        for i, d in enumerate(by_s):
+            mms([(A("ps%d" % (i % 2), L * (i // 2), L * (i // 2) + L), A("ID"), A("X", L * d, L * d + L), True, True)])
+        for j, (lo, hi) in enumerate(chunks):
+            bank = ("ps7", "ps2", "ps7")[j]
+            for i in range(lo, hi):
+                d = order_c[i]
+                if d in by_s:
+                    k = by_s.index(d)
+                    act(A("KA", L * i, L * i + L), I(A("KW"), sl16(P, d)))
+                    tt(A("PC", L * i, L * i + L), A("KA", L * i, L * i + L), A("ps%d" % (k % 2), L * (k // 2), L * (k // 2) + L), OP.mult)
+                else:
+                    tt(A("PC", L * i, L * i + L), I(A("KW"), sl16(P, d)), A("X", L * d, L * d + L), OP.mult)
+            conv(A(bank, 144 + 16 * lo, 144 + 16 * hi), "ZA", lambda a: A("PC", L * lo + a, L * hi, 16))
+            dests = [d for d in order_c[lo:hi] if d != r]
+            if dests:
+                ts(sl16("sC%d" % t, lo, len(dests)), sl16(bank, 9 + lo, len(dests)), BIAS, OP.add)
+                deal("aC%d" % t, dests, lambda d: [sl16("sC%d" % t, order_c.index(d))], lambda d: sl16("lC%d" % t, slot(d)))
+
+        best, low11, N0, N1 = new("n"), new("n"), new("f"), new("f")
+        Po, mine = sl16("PF", r), sl16(Pn, r)
+
+        def moves(d, sign):
+            x, y = new("f", d[2]), new("f", d[2])
+            tt(x, d, sign, OP.mult)
+            ts(y, x, 0.0, OP.is_gt)
+            return x, y
+
+        if r == lead:
+            landed("aL%d" % t, A("lL%d" % t))
+            x, y = moves(tree(lambda o: tt(o, A("ps6", 80, 112), cut(hT, 16, 48), OP.subtract), "lL%d" % t, 32), cut(sign, 16, 48))
+            tt(x, y, cand, OP.mult)
+            tt(N0, cut(x, 0, 16), cut(x, 16, 32), OP.max)
+            tt(best, N0, Po, OP.max)
+        else:
+            landed("aU%d" % t, A("lU%d" % t))
+            dU, x = tree(lambda o: tt(o, A("ps6", 64, 80), cut(hT, 0, 16), OP.subtract), "lU%d" % t, 16), new("f")
+            tt(x, dU, cut(sign, 0, 16), OP.mult)
+            ts(A("OW", 1, 17), x, 0.0, OP.is_gt)
+            tt(A("OG"), I(A("OW", 0, 17), ao), A("MK"), OP.mult)
+            conv(A("ps5", 128, 144), "ZA", lambda a: A("OG", a, L, 16))
+            tt(N0, e3, A("ps5", 128, 144), OP.mult)
+            tt(N1, N0, Po, OP.max)
+            landed("aC%d" % t, A("lC%d" % t))
+            x, y = moves(tree(lambda o: tt(o, sl16("ps7", 8 + nc), cut(hT, 16, 32), OP.subtract), "lC%d" % t, 16), cut(sign, 16, 32))
+            tt(x, y, cut(cand, 0, 16), OP.mult)
+            tt(best, x, N1, OP.max)
+        ts(low11, best, 2047, OP.bitwise_and)
+        if r == lead:
+            mine = A("H%d" % lead)
+            for b in range(2):
+                copy(cut(mine, 8 * b, 8 * b + 8), cut(low11, b, 16, 2))
+        else:
+            copy(mine, low11)
+        share("aS%d" % t if r == lead else "aD%d" % t, mine, lambda d: mine)
+        if lead is not None and r != lead:
+            landed("aS%d" % t, A("H%d" % lead))
+        landed("aD%d" % t, [sl16(Pn, d)[1][0] for d in peers if d != lead])
+
+    dmas("S", [(hbm("yc"), A("YC"))], 128, 192)
+    copy(A("YP"), A("P%d" % R))
+    dmas("Y", [(hbm("yp"), A("YP"))], 128, 512)
+    return totals
+
+
+def arrange(steps):
+    n = len(steps)
+    follow = [[] for _ in range(n)]
+    for i, x in enumerate(steps):
+        for j in x["hard"] | x["soft"]:
+            follow[j].append(i)
+    flight = [START + x["rows"][0] / 16 * (ROW + x["rows"][1] * BYTE) if x["rows"] else 0.0 for x in steps]
+    left = [len(x["hard"] | x["soft"]) for x in steps]
+    topo_order, todo, count = [], [i for i in range(n) if not left[i]], list(left)
+    while todo:
+        i = todo.pop()
+        topo_order.append(i)
+        for j in follow[i]:
+            count[j] -= 1
+            if not count[j]:
+                todo.append(j)
+    way = [0.0] * n
+    for i in reversed(topo_order):
+        way[i] = steps[i]["time"] + flight[i] + SIGNAL + max([way[j] for j in follow[i]] or [0.0])
+    free, engines, bank, begin, end, ready = {}, {}, {}, [0.0] * n, [0.0] * n, {}
+
+    def release(i):
+        x = steps[i]
+        if x["q"]:
+            ready.setdefault((x["rank"], x["q"]), []).append(i)
+        else:
+            finish(i, max(end[j] for j in x["hard"]))
+
+    def finish(i, at):
+        end[i] = at
+        for j in follow[i]:
+            left[j] -= 1
+            if not left[j]:
+                release(j)
+
+    def earliest(i):
+        x = steps[i]
+        times = [free.get((x["rank"], x["q"]), 0.0)] + [end[j] + SIGNAL for j in x["hard"]]
+        for b in x["banks"]:
+            times += [end[j] + SIGNAL for q, j in bank.get((x["rank"], b), {}).items() if q != x["q"]]
+        return max(times)
+
+    for i in [i for i in range(n) if not left[i]]:
+        release(i)
+    order = []
+    while any(ready.values()):
+        pick = None
+        for key, waiting in ready.items():
+            if waiting:
+                at = {i: earliest(i) for i in waiting}
+                first = min(waiting, key=lambda i: at[i] - way[i])
+                fits = [i for i in waiting if at[i] + steps[i]["time"] <= at[first] + SIGNAL and i != first]
+                if fits:
+                    first = min(fits, key=lambda i: (at[i] - way[i]))
+                if pick is None or at[first] < pick[0]:
+                    pick = (at[first], first, key)
+        at, i, key = pick
+        x = steps[i]
+        ready[key].remove(i)
+        order.append(i)
+        for b in x["banks"]:
+            seen = bank.setdefault((x["rank"], b), {})
+            x["hard"] = x["hard"] | {j for q, j in seen.items() if q != x["q"]}
+            seen[x["q"]] = i
+        free[key] = at + x["time"]
+        done = free[key]
+        if x["rows"]:
+            done = max(done + START, engines.get(x["rank"], 0.0)) + flight[i] - START
+            engines[x["rank"]] = done
+        finish(i, done)
+    return order
 
 
 def rank_program(g, core, T, topo):
     r = T.rank_of(core)
     if r is None:
         return
+    if not PLAN:
+        steps, arrivals = [], {}
+        totals = [describe(d, T.cores, topo, steps, arrivals) for d in range(N)]
+        for key in [k for k in arrivals if len(k) == 2]:
+            x = steps[arrivals[key + ("step",)]]
+            x["hard"] = x["hard"] | {i for i, _ in arrivals[key]}
+            x["sem"] = (key[1], sum(k for _, k in arrivals[key]))
+            totals[key[0]][key[1]] = x["sem"][1]
+        PLAN.update(steps=steps, order=arrange(steps), totals=totals)
+    steps, totals = PLAN["steps"], dict(PLAN["totals"][r])
     eng = {"V": g.vector, "S": g.scalar, "P": g.tensor, "G": g, "Y": g.sync}
-    cnt = {"V": 0, "S": 0, "P": 0, "G": 0}
+    call = {"tensor_copy": g.vector.tensor_copy, "tensor_tensor": g.vector.tensor_tensor, "tensor_scalar": g.vector.tensor_scalar,
+            "tensor_reduce": g.vector.tensor_reduce, "memset": g.vector.memset, "activation": g.scalar.activation,
+            "matmul": g.tensor.matmul, "iota": g.iota}
     known = {q: {} for q in eng}
-    hist = {}
-    totals = {}
-    ndma = [0]
+    count = {q: 0 for q in "VSPG"}
+    mark = {}
 
-    def A(name, lo=0, hi=None, step=1):
-        if hi is None:
-            hi = SCRATCH[name][1][1]
-        ap = T[name][:, lo:hi] if step == 1 else T[name][:, lo:hi:step]
-        return (ap, [(name, lo, hi)])
-
-    def I(win, off):
-        return (win[0].indirect(off[0]), win[1] + off[1])
+    def ap(a):
+        if not isinstance(a, tuple):
+            return a
+        if len(a[0]) == 3:
+            return T[a[0][0][0]][a[0][0][1]].indirect(T[a[0][1][0]][a[0][1][1]])
+        return T[a[0][0]][a[0][1]]
 
     def wait(q, sem, val):
         if known[q].get(sem, 0) < val:
             eng[q].wait_ge(T.sem[sem], val)
             known[q][sem] = val
 
-    def order(q, reads, writes, mark, dma=False):
-        need = {}
-        acc = [(k, False) for k in reads] + [(k, True) for k in writes]
-        for (name, lo, hi), wr in acc:
-            psum = name.startswith("ps")
-            for (l2, h2, w2, q2, s2, v2) in hist.get(name, []):
-                if q2 == q and not dma:
-                    if q == "P" or wr or not w2 or h2 <= lo or hi <= l2:
-                        continue
-                elif not psum and (h2 <= lo or hi <= l2 or not (wr or w2)):
-                    continue
-                need[s2] = max(need.get(s2, 0), v2)
-        for s2 in need:
-            wait(q, s2, need[s2])
-        for (name, lo, hi), wr in acc:
-            hist.setdefault(name, []).append((lo, hi, wr, "dma" if dma else q, mark[0], mark[1]))
-
-    def op(q, fn, out, ins, more=()):
-        cnt[q] += 1
-        reads = [k for a in ins if isinstance(a, tuple) for k in a[1]] + out[1][1:]
-        order(q, reads, out[1][:1] + list(more), ("q" + q, cnt[q]))
-        fn().then_inc(T.sem["q" + q], 1)
-
-    def ap(x):
-        return x[0] if isinstance(x, tuple) else x
-
-    def copy(out, a):
-        op("V", lambda: g.vector.tensor_copy(out[0], a[0]), out, [a])
-
-    def tt(out, a, b, o):
-        op("V", lambda: g.vector.tensor_tensor(out[0], a[0], b[0], o), out, [a, b])
-
-    def ts(out, a, s1, o0, s2=None, o1=None):
-        if o1 is None:
-            op("V", lambda: g.vector.tensor_scalar(out[0], a[0], ap(s1), None, o0), out, [a, s1])
-        else:
-            op("V", lambda: g.vector.tensor_scalar(out[0], a[0], ap(s1), ap(s2), o0, o1), out, [a, s1, s2])
-
-    def red(out, a, o):
-        op("V", lambda: g.vector.tensor_reduce(out[0], a[0], AxisListType.X, o), out, [a])
-
-    def fill(out, v):
-        op("V", lambda: g.vector.memset(out[0], v), out, [])
-
-    def act(out, a, fn=AF.Copy, bias=None, scale=None, acc=None):
-        kw = {}
-        if bias is not None:
-            kw["bias"] = ap(bias)
-        if scale is not None:
-            kw["scale"] = ap(scale)
-        if acc is not None:
-            kw["accum_out"] = acc[0]
-        op("S", lambda: g.scalar.activation(out[0], a[0], fn, **kw), out, [a, bias, scale], acc[1] if acc else ())
-
-    def mm(out, lhs, rhs, start, stop):
-        op("P", lambda: g.tensor.matmul(out[0], lhs[0], rhs[0], start, stop), out, [lhs, rhs])
-
-    def iota(out, pattern, base, mult):
-        if SCRATCH[out[1][0][0]][2] == "int32":
-            op("G", lambda: g.iota(out[0], pattern, base, mult), out, [])
-        else:
-            op("G", lambda: g.iota(out[0], pattern, base, mult, allow_small_or_imprecise_dtypes=True), out, [])
-
-    def dma(q, out, a, sem=None, val=None):
-        if sem is None:
-            sem, val = "d%d" % ndma[0], 16
-            ndma[0] += 1
-        order(q, a[1], out[1], (sem, val), dma=True)
-        eng[q].dma_start(out[0], a[0]).then_inc(T.sem[sem], 16)
-        totals[sem] = val
-
-    def conv(out, z, src, blocks=range(16)):
-        for i in blocks:
-            mm(out, A(z, 15 - i, 143 - i), src(i), i == 0, i == 15)
-
-    peers = [d for d in range(N) if d != r]
-    lanes = topo.engines(core, T.cores[peers[0]])
-    far = [d for d in peers if topo.die(T.cores[d]) != topo.die(core)]
-    near = [d for d in peers if d not in far]
-    masks = {}
-    for group, pool in ((far, lanes[0::2]), (near, lanes[1::2])):
-        for i, d in enumerate(group):
-            masks[d] = (1 << pool[2 * i]) | (1 << pool[2 * i + 1])
-    totals["sent"] = 0
-
     def dst(d):
         rid, pid, _ = topo.addr(T.cores[d])
         return DstId(rid=rid, pnc=pid)
 
-    def slot(d):
-        return (r - d - 1) % N
+    def needs(i):
+        out = []
+        for j in steps[i]["hard"]:
+            if steps[j]["q"]:
+                out.append(mark[j])
+            else:
+                out.append(steps[j]["sem"])
+        return out
 
-    def landed(sem, val, keys):
-        totals[sem] = val
-        for name, lo, hi in keys:
-            hist.setdefault(name, []).append((lo, hi, True, "dma", sem, val))
-
-    def deal(sem, src, land, w):
-        order("G", A(src)[1], [], ("sent", 0), dma=True)
-        g.remote_dma_fused([RemoteDMATransfer(dst_ids=[dst(d)], dma_engine_mask=masks[d], remote_sem=T.sem[sem],
-                                              src=A(src, w * d, w * d + w)[0], dst=A(land, w * slot(d), w * slot(d) + w)[0])
-                            for d in peers], local_sem=T.sem.sent)
-        totals["sent"] += 2 * len(peers)
-        landed(sem, 2 * len(peers), A(land)[1])
-
-    def share(sem, src, land, keys, own=None):
-        order("G", src[1], [], ("sent", 0), dma=True)
-        g.remote_dma_fused([RemoteDMATransfer(dst_ids=[dst(d) for d in peers], dma_engine_mask=topo.mask(core, T.cores[peers[0]]),
-                                              remote_sem=T.sem[sem], srcs=[src[0]], dsts=[land(d)[0] for d in peers])],
-                           local_sem=T.sem.sent)
-        totals["sent"] += len(lanes)
-        n = len(lanes) * len(peers)
-        if own:
-            n += 16
-            dma("Y", own, src, sem, n)
-        landed(sem, n, keys)
-
-    def tree(out, cv, land, w, scale=None):
-        if scale:
-            ts(A(cv, 0, 7 * w), A(land), scale, OP.mult)
-        else:
-            copy(A(cv, 0, 7 * w), A(land))
-        tt(A("tr", 0, 4 * w), A(cv, 0, 4 * w), A(cv, 4 * w, 8 * w), OP.add)
-        tt(A("tr", 4 * w, 6 * w), A("tr", 0, 2 * w), A("tr", 2 * w, 4 * w), OP.add)
-        tt(out, A("tr", 4 * w, 5 * w), A("tr", 5 * w, 6 * w), OP.add)
-
-    def ext(t):
-        return (t, [])
-
-    def expand(t):
-        for k in range(16):
-            act(A("XE%d" % t, k, 2048, 16), A("X", L * t, L * t + 128))
-
-    def clear_window():
-        iota(A("W1"), [[0, W]], 0, 0)
-
-    dma("Y", A("PA"), ext(T.pa[:]))
-    dma("Y", A("X", 0, L), ext(T.xv[:, 0:L]))
-    dma("S", A("BC", 0, Q), ext(T.bt[:]))
-    dma("S", A("BC", Q, 2 * Q), ext(T.co[:]))
-    dma("Y", A("CD"), ext(T.cd[:]))
-    dma("Y", A("K"), ext(T.kc[:]))
-    dma("Y", A("X", L, V), ext(T.xv[:, L:V]))
-
-    cA, cG, c15, cT, cW, cC, cZ, cU, cV = [A("col", i, i + 1) for i in range(9)]
-    row6, row7 = A("I16", 6, 7), A("I16", 7, 8)
-    BN, DN, VN, ZS = A("ST", 0, 2), A("ST", 2, 4), A("ST", 16, 32), A("ST", 32, 48)
-    iota(A("ii", 0, 1), [[0, 1]], 0, 1)
-    iota(A("i1"), [[1, 144]], 0, -1)
-    iota(A("i3"), [[0, 16], [1, 16]], 0, 0)
-    iota(A("i4"), [[1, 16], [0, 16]], 0, 0)
-    iota(A("i5"), [[1, 256]], 0, 0)
-    iota(A("KP"), [[0, 2], [16384, 16]], 0, 0)
-    iota(A("CP", 6 * Q, 7 * Q), [[1, Q]], -Q // 2, 0)
-    iota(A("META", 0, C // 3), [[0, C // 3]], 1, 0)
-    fill(A("META", C // 3, 2 * C // 3), 1.0)
-    act(A("META", 2 * C // 3, C), A("META", C // 3, 2 * C // 3))
-    ts(A("ii", 1, 2), A("ii", 0, 1), 15, OP.bitwise_and)
-    ts(A("ii", 2, 3), A("ii", 0, 1), 4, OP.arith_shift_right)
-    copy(A("col", 0, 2), A("ii", 1, 3))
-    ts(c15, cA, -1.0, OP.mult, 15.0, OP.add)
-    ts(A("I16"), A("i3", 0, 16), cA, OP.is_equal)
-    ts(A("BK"), A("i4", 0, 128), cG, OP.is_equal)
-    ts(A("ZA"), A("i1"), c15, OP.is_equal)
-    ts(A("ID"), A("i1", 0, 128), 0.0, OP.is_equal)
-    ts(A("JJ"), A("i5"), A("I16", 0, 1), OP.mult, 1.0 / 512, OP.mult)
-    ts(VN, A("i3", 0, 16), 16.0, OP.mult, cA, OP.add)
-    for a in range(16):
-        ts(A("BA", 128 * a, 128 * a + 128), A("BK"), A("I16", a, a + 1), OP.mult)
-    ts(BN, A("ST", 16 + 2 * r, 18 + 2 * r), -1.0 / 512, OP.mult, 0.25, OP.add)
-    ts(DN, A("ST", 16 + 2 * r, 18 + 2 * r), float(V), OP.add)
-    copy(A("P0"), A("PA"))
-
-    def own_lane(i, a):
-        return A("e", 2 * i + a, 2 * i + a + 1)
-
-    def first_keys(t):
-        s = A("P%d" % t, 16 * t, 16 * t + 16)
-        copy(A("S16"), s)
-        copy(A("SF"), s)
-        mm(A("ps4", 0, 256), A("BK"), A("JJ"), True, False)
-        for a in range(16):
-            mm(A("ps4", a, 256, 16), A("BA", 128 * a, 128 * a + 128), A("S16"), False, a == 15)
-
-    def first_slots(t):
-        sf = [A("SF", 2 * r + a, 2 * r + a + 1) for a in range(2)]
-        for a in range(2):
-            act(own_lane(0, a), sf[a], AF.Identity, bias=A("ST", a, a + 1), scale=-1.0)
-        act(A("e", 2, 4), A("SF", 2 * r, 2 * r + 2), AF.Abs, bias=-(L * t + 127.5))
-        for a in range(2):
-            act(A("EK", L * a, L * a + L), A("ps4", 0, 256), AF.Abs, bias=own_lane(0, a))
-        act(A("e", 4, 6), A("e", 2, 4), AF.Relu, bias=128.0, scale=-1.0)
-        for a in range(2):
-            act(A("EK2", L * a, L * a + L), A("EK", L * a, L * a + L), AF.Relu, bias=0.249, scale=-1.0, acc=own_lane(3, a))
-        for a in range(2):
-            act(own_lane(4, a), sf[a], AF.Identity, bias=A("ST", 2 + a, 3 + a), scale=-1.0)
-        for a in range(2):
-            act(own_lane(5, a), own_lane(3, a), AF.Sign, bias=own_lane(2, a))
-        for a in range(2):
-            act(own_lane(6, a), own_lane(5, a), AF.Identity, bias=sf[a], scale=own_lane(4, a))
-
-    def first_send(t):
-        src, place = A("sF%d" % t, 0, 2), A("lF%d" % t, 2 * r, 2 * r + 2)
-        copy(src, A("e", 12, 14))
-        share("aF%d" % t, src, lambda d: place, A("lF%d" % t)[1], place)
-
-    first_keys(0)
-    first_slots(0)
-    expand(0)
-    copy(A("CP", 0, 2 * Q), A("BC"))
-    ts(cU, cA, float(Q), OP.mult, Q / 2, OP.add)
-    for i in range(2):
-        tt(A("ps%d" % (1 + i), 0, Q), A("BC", i * Q, i * Q + Q), A("CP", i * Q, i * Q + Q), OP.subtract)
-    first_send(0)
-    for i in range(2):
-        copy(A("CP", (2 + i) * Q, (3 + i) * Q), A("ps%d" % (1 + i), 0, Q))
-    ts(A("CP", 7 * Q, 8 * Q), A("CP", 6 * Q, 7 * Q), 0.0, OP.mult, cU, OP.add)
-    for i in range(2):
-        tt(A("CP", (4 + i) * Q, (5 + i) * Q), A("ps%d" % (1 + i), 0, Q), A("CP", (2 + i) * Q, (3 + i) * Q), OP.subtract)
-    msem = "d%d" % ndma[0]
-    ndma[0] += 1
-    order("Y", A("CP")[1] + A("K")[1], A("META")[1], (msem, 128), dma=True)
-    for row, part in ((0, 0), (1, 2), (2, 4), (3, 1), (4, 3), (5, 5), (6, 6), (8, 7)):
-        g.sync.dma_start(T.META[row:128:16, :], T.CP[:, part * Q:part * Q + Q]).then_inc(T.sem[msem], 16)
-    totals[msem] = 128
-
-    def selectors(h):
-        if not h:
-            red(cT, A("I16", 0, 3), OP.add)
-            red(cW, A("I16", 3, 6), OP.add)
-            tt(cC, A("I16", 8, 9), row6, OP.add)
-            ts(A("ZT"), A("i1"), c15, OP.is_equal, cT, OP.mult)
-            ts(cV, cW, 2.0 ** -25, OP.mult)
-        else:
-            ts(A("ZW"), A("i1"), c15, OP.is_equal, cV, OP.mult)
-            ts(A("ZC"), A("i1"), c15, OP.is_equal, cC, OP.mult)
-            fill(A("SC"), 0.125)
-
-    iota(A("ZV"), [[1, 16], [16, 16]], 1, 0)
-    iota(A("AC"), [[1, L]], 1, 0)
-    dma("Y", (T.ZV[6:128:16, :], A("ZV")[1]), (T.AC[6:128:16, :], A("AC")[1]))
-    clear_window()
-    for name in ("IZ", "KC", "MB", "SB", "OW"):
-        iota(A(name, 0, 16), [[0, 16]], 0, 0)
-    iota(A("SW", 0, 2), [[2, 2]], -1, 0)
-    iota(A("SW", 2, 16), [[0, 14]], 0, 0)
-    iota(A("SW", 16, 18), [[0, 2]], 1, 0)
-    iota(A("SW", 18, 1056), [[0, 1038]], 0, 0)
-
-    def last_constants():
-        ts(A("ZL"), A("i1"), c15, OP.is_equal, row6, OP.mult)
-        act(A("EK", 0, L), A("i3"), AF.Abs, bias=cA, scale=-1.0)
-        act(A("IZ", 16, 272), A("EK", 0, L), AF.Relu, bias=1.0, scale=-1.0)
-        if r < R:
-            act(cU, cA, AF.Identity, bias=1.0, scale=16.0)
-            act(ZS, A("i3", 0, 16), AF.Identity, bias=cU)
-            act(VN, VN, AF.Identity, bias=float(L * r))
-
-    for t in range(R):
-        P, Pn = "P%d" % t, "P%d" % (t + 1)
-        s = A(P, 16 * t, 16 * t + 16)
-        XE = "XE%d" % t
-        pX, pI, pS = A("ps0", 0, 256), A("ps1", 0, 256), A("ps2", 0, 256)
-
-        def parents_x():
-            act(A("XS"), I(A("X"), s))
-            mm(pX, A("ID"), A("XS"), True, True)
-
-        def own_side(lo, hi):
-            tt(A("PI", 16 * lo, 16 * hi), I(A("K"), A("E", lo, hi)), A(XE, 16 * lo, 16 * hi), OP.mult)
-            conv(pI, "ZA", lambda b: A("PI", 256 * b, 256 * b + 256), range(lo // 16, hi // 16))
-
-        spare = ("ps3", "ps5", "ps6", "ps7")
-        for j, bank in enumerate(spare):
-            for k in range(16):
-                mm(A(bank, k, 512, 16), A("ID"), A("X", L * t + 128 + 32 * j, L * t + 160 + 32 * j), True, True)
-        copy(A("E"), I(A("CD"), s))
-        if t:
-            parents_x()
-        act(A("KG", 0, 2048), I(A("K"), A("E", 0, 128)))
-        if not t:
-            parents_x()
-        act(A("KG", 2048, 4096), I(A("K"), A("E", 128, 256)))
-        own_side(0, 64)
-        if t:
-            first_keys(t)
-            first_slots(t)
-        own_side(64, 128)
-        for a in range(2):
-            copy(A("EO", a, 32, 2), A("E", 2 * r + a, L, 16))
-        act(A("MG"), I(A("META"), A("EO")))
-        if not t:
-            last_constants()
-        cu, fo, sh, sl, upu, ao = [A("u", 16 * i, 16 * i + 16) for i in range(6)]
-        n0, n1, n2, n3, n4 = [A("n", 16 * i, 16 * i + 16) for i in range(5)]
-        for h in range(2):
-            if not t:
-                selectors(h)
-            for k in range(16):
-                tt(A("PS", 2048 * h + k, 2048 * h + 2048, 16), A("KG", 2048 * h + k, 2048 * h + 2048, 16),
-                   A("ps0", 128 * h, 128 * h + 128), OP.mult)
-            conv(pS, "ZA", lambda b: A("PS", 256 * b, 256 * b + 256), range(8 * h, 8 * h + 8))
-        if t:
-            first_send(t)
-        for j, bank in enumerate(spare):
-            cuts = (0, 512) if j < 3 else (0, 256, 512)
-            for lo, hi in zip(cuts, cuts[1:]):
-                c0 = 2048 + 512 * j
-                tt(A("PI", c0 + lo, c0 + hi), A("KG", c0 + lo, c0 + hi), A(bank, lo, hi), OP.mult)
-                conv(pI, "ZA", lambda b: A("PI", 256 * b, 256 * b + 256), range((c0 + lo) // 256, (c0 + hi) // 256))
-        ts(A("sI%d" % t, 0, 512, 2), pS, BIAS, OP.add)
-        ts(A("sI%d" % t, 1, 512, 2), pI, BIAS, OP.add)
-        deal("aI%d" % t, "sI%d" % t, "lI%d" % t, 64)
-
-        thr, pay, dS, dI, sc, tq, uq = [A("f", 32 * i, 32 * i + 32) for i in range(7)]
-        mcol = lambda i: A("f", 256 + i, 257 + i)
-        conv(A("ps3", 0, 32), "ZT", lambda b: A("MG", 32 * b, 32 * b + 32))
-        conv(A("ps0", 0, 32), "ZW", lambda b: A("MG", 32 * b, 32 * b + 32))
-        conv(A("ps0", 32, 64), "ZC", lambda b: A("MG", 32 * b, 32 * b + 32), range(15))
-        mm(A("ps0", 32, 64), A("ID"), A("KP"), False, False)
-        conv(A("ps0", 32, 64), "ZC", lambda b: A("MG", 32 * b, 32 * b + 32), [15])
-        copy(I(A("W1"), A("lF%d" % t)), A("ZV"))
-        act(thr, A("ps3", 0, 32), AF.Identity, bias=7 * BIAS + 0.5)
-        act(A("UB", 0, 1280), I(A("W1"), A(P, 0, 80)))
-        copy(n0, s)
-        copy(A("PF"), A(P))
-        ts(n1, n0, 4, OP.arith_shift_right)
-        ts(n2, n0, 15, OP.bitwise_and)
-        copy(A("UB", V, W), A("W1", L * r, L * r + L))
-        copy(sh, n1)
-        copy(sl, n2)
-        act(A("UB", 1280, V), I(A("W1"), A(P, 80, 128)))
-        tt(A("cvI", 448, 512, 2), A("ps2", 32 * r, 32 * r + 32), thr, OP.subtract)
-        tt(A("cvI", 449, 512, 2), A("ps1", 32 * r, 32 * r + 32), thr, OP.subtract)
-        for b in range(2):
-            mm(A("ps%d" % (1 + b)), A("ID"), A("X", 1024 + 512 * b, 1536 + 512 * b), True, True)
-        if not t:
-            ts(A("ZY"), A("i1"), c15, OP.is_equal, row7, OP.mult)
-        conv(A("ps5", 0, 80), "ZY", lambda a: A("UB", a, 1280, 16))
-        conv(A("ps5", 80, 144), "ZY", lambda a: A("UB", 1280 + a, W, 16))
-
-        copy(A("ps6", 0, 256), A("lI%d" % t, 0, 256))
-        copy(A("cvI", 256, 448), A("lI%d" % t, 256, 448))
-        tt(A("ps7", 0, 128), A("ps6", 0, 128), A("cvI", 256, 384), OP.add)
-        tt(A("tr", 0, 128), A("ps6", 128, 256), A("cvI", 384, 512), OP.add)
-        tt(A("tr", 128, 256), A("ps7", 0, 128), A("tr", 0, 128), OP.add)
-        tt(A("f", 64, 128), A("tr", 128, 192), A("tr", 192, 256), OP.add)
-        tt(tq, A("f", 64, 128, 2), A("f", 65, 128, 2), OP.mult)
-        ts(pay, A("f", 64, 128, 2), 0.0, OP.is_lt, 8192.0, OP.mult)
-        tt(A("SC", 1, 33), tq, A("ps0", 0, 32), OP.max)
-        tt(pay, pay, A("ps0", 32, 64), OP.add)
-        for a in range(2):
-            red(mcol(a), A("SC", 17 * a, 17 * a + 17), OP.min)
-        for a in range(2):
-            ts(A("f", 160 + 16 * a, 176 + 16 * a), A("SC", 1 + 16 * a, 17 + 16 * a), mcol(a), OP.is_gt, 2.0 ** 23, OP.mult)
-        tt(uq, tq, pay, OP.add)
-        for a in range(2):
-            red(A("sB%d" % t, a, a + 1), A("f", 192 + 16 * a, 208 + 16 * a), OP.min)
-        msg, lB = A("sB%d" % t, 0, 2), A("lB%d" % t)
-        place = A("lB%d" % t, 2 * r, 2 * r + 2)
-        share("aB%d" % t, msg, lambda d: place, lB[1], place)
-
-        okN, e1, e2, val, base, ya, dl, dU, dC, e3 = [A("h", 32 + 16 * i, 48 + 16 * i) for i in range(10)]
-        Po = A("PF", 16 * r, 16 * r + 16)
-        copy(A("G"), I(A("PF"), sh))
-        tt(A("UX"), I(A("I16"), sl), A("G"), OP.mult)
-        conv(A("ps4", 64, 80), "ZA", lambda b: A("UX", 16 * b, 16 * b + 16))
-        if r == t:
-            conv(A("ps4", 16, 32), "ZA", lambda a: A("UX", a, L, 16))
-        if r == t:
-            ts(okN, A("lF%d" % t), float(V), OP.is_lt)
-            tt(e2, ZS, okN, OP.mult)
-            ts(A("UU", 0, 128), A("ps5", 0, 128), 15.0, OP.add)
-            ts(A("UU", 128, 144), e2, 15.0, OP.add)
-            ts(n3, e2, 15.0, OP.add)
-        else:
-            ts(A("UU"), A("ps5", 0, 144), 15.0, OP.add)
-            ts(n3, A("ps5", 128, 144), 15.0, OP.add)
-        copy(upu, A("ps4", 64, 80))
-        act(A("XS"), I(A("X"), upu))
-        mm(A("ps6", 256, 512), A("ID"), A("XS"), True, True)
-        conv(A("ps4", 0, 16), "ZL", lambda a: A("UB", L * r + a, L * r + L, 16))
-        if r != t:
-            conv(A("ps4", 16, 32), "ZL", lambda a: A("UB", V + a, W, 16))
-
-        ts(n0, lB, 8191, OP.bitwise_and)
-        ts(n1, lB, 13, OP.arith_shift_right, 1025, OP.bitwise_and)
-        copy(cu, n0)
-        copy(fo, n1)
-        copy(A("KC", 16, 272), I(A("K"), cu))
-        act(A("MB", 16, 272), I(A("META"), cu))
-        mine_u = A("UU", 16 * r, 16 * r + 16)
-        for b in range(2):
-            act(A("KA", 512 * b, 512 * b + 512), I(A("KC"), A("UU", 64 + 32 * b, 96 + 32 * b)))
-        act(e1, A("ps4", 0, 16), AF.Identity, bias=float(L * t - 1))
-        act(e3, A("ps4", 16, 32), AF.Identity, bias=0.0 if r == t else float(L * t - 1))
-        tt(A("PU"), A("KC", 16, 272), A("ps6", 256, 512), OP.mult)
-        conv(A("ps6", 0, 16), "ZA", lambda b: A("PU", b, L, 16))
-        conv(A("ps3", 0, 16), "ZT", lambda b: A("MB", 16 + b, 272, 16))
-        act(A("SB", 16, 272), I(A("SW", 0, 1040), fo))
-        act(A("h", 0, 16), A("ps3", 0, 16), AF.Identity, bias=7 * BIAS + 0.5)
-        act(A("MB", 272, 528), I(A("MB", 0, 272), mine_u))
-        act(A("SB", 272, 528), I(A("SB", 0, 272), mine_u))
-        tt(A("PC", 0, 384), I(A("KC"), A("UU", 0, 24)), A("X", 0, 384), OP.mult)
-        ts(A("sU%d" % t), A("ps6", 0, 16), BIAS, OP.add)
-        share("aU%d" % t, A("sU%d" % t), lambda d: A("lU%d" % t, 16 * slot(d), 16 * slot(d) + 16), A("lU%d" % t)[1])
-        tt(A("PC", 384, 1024), I(A("KC"), A("UU", 24, 64)), A("X", 384, 1024), OP.mult)
-        conv(A("ps7", 0, 64), "ZA", lambda a: A("PC", a, 1024, 16))
-        for b in range(2):
-            tt(A("PC", 1024 + 512 * b, 1536 + 512 * b), A("KA", 512 * b, 512 * b + 512), A("ps%d" % (1 + b)), OP.mult)
-        conv(A("ps7", 64, 128), "ZA", lambda a: A("PC", 1024 + a, V, 16))
-        conv(A("ps5", 256, 272), "ZY", lambda b: A("SB", 16 + b, 272, 16))
-        conv(A("ps0", 0, 16), "ZT", lambda a: A("MB", 272 + a, 528, 16))
-        conv(A("ps4", 48, 64), "ZY", lambda a: A("SB", 272 + a, 528, 16))
-        ts(n4, n3, 4, OP.arith_shift_right)
-        tt(dl, e1, Po, OP.subtract)
-        tt(val, e3, Po, OP.subtract)
-        copy(ao, n4)
-        if r == t:
-            tt(e2, e1, VN, OP.not_equal)
-            tt(dl, dl, e2, OP.mult)
-        ts(A("sC%d" % t), A("ps7", 0, 128), BIAS, OP.add)
-        deal("aC%d" % t, "sC%d" % t, "lC%d" % t, 16)
-
-        act(A("MK"), I(A("IZ"), A("UU", 128, 144)))
-        act(A("h", 16, 32), A("ps0", 0, 16), AF.Identity, bias=7 * BIAS + 0.5)
-        if t + 1 < R:
-            expand(t + 1)
-        tt(A("cvU", 112, 128), A("ps6", 0, 16), A("h", 0, 16), OP.subtract)
-        tree(dU, "cvU", "lU%d" % t, 16)
-        tt(dU, dU, A("ps5", 256, 272), OP.mult)
-        tt(A("cvC", 112, 128), A("ps7", 16 * r, 16 * r + 16), A("h", 16, 32), OP.subtract)
-        ts(A("OW", 1, 17), dU, 0.0, OP.is_gt)
-        tt(A("OG"), I(A("OW", 0, 17), ao), A("MK"), OP.mult)
-        conv(A("ps6", 16, 32), "ZA", lambda a: A("OG", a, L, 16))
-
-        tree(dC, "cvC", "lC%d" % t, 16)
-        tt(dC, dC, A("ps4", 48, 64), OP.mult)
-        ts(dC, dC, 0.0, OP.is_gt)
-        tt(dC, dC, dl, OP.mult)
-        tt(ya, val, dC, OP.subtract)
-        tt(base, dC, Po, OP.add)
-        tt(ya, ya, A("ps6", 16, 32), OP.mult)
-        tt(base, base, ya, OP.add)
-        mine = A(Pn, 16 * r, 16 * r + 16)
-        copy(mine, base)
-        lead = t + 1 if t + 1 < R else None
-        share("aS%d" % t if r == lead else "aD%d" % t, mine, lambda d: mine, [])
-        if r == lead:
-            del totals["aS%d" % t]
-        elif lead is not None:
-            landed("aS%d" % t, len(lanes), [(Pn, 16 * lead, 16 * lead + 16)])
-        rest = [d for d in peers if d != lead]
-        landed("aD%d" % t, len(lanes) * len(rest), [(Pn, 16 * d, 16 * d + 16) for d in rest])
-        if t + 1 < R:
-            clear_window()
-
-        if not t:
-            tt(cZ, cW, row7, OP.add)
-            ts(A("ZZ"), A("i1"), c15, OP.is_equal, cZ, OP.mult)
-        tt(A("AC"), I(A("SW", 16, 1056), fo), A("MB", 16, 272), OP.mult)
-        if r != t:
-            ts(okN, A("lF%d" % t), float(V), OP.is_lt)
-        conv(A("ps3", 64, 80), "ZZ", lambda a: A("AC", 16 * a, 16 * a + 16))
-        tt(e1, A("ps3", 64, 80), okN, OP.mult)
-        ts(A("YC", 16 * t, 16 * t + 16), e1, -1.0, OP.add)
-
-    dma("S", ext(T.yc[:]), A("YC"))
-    copy(A("YP"), A("P%d" % R))
-    dma("Y", ext(T.yp[:]), A("YP"))
-    for q in cnt:
-        totals["q" + q] = cnt[q]
+    for i in PLAN["order"]:
+        x = steps[i]
+        if x["rank"] != r:
+            continue
+        q, need = x["q"], {}
+        for sem, val in needs(i):
+            need[sem] = max(need.get(sem, 0), val)
+        for sem in need:
+            wait(q, sem, need[sem])
+        for name, args, kw in x["calls"]:
+            if name == "remote":
+                g.remote_dma_fused([RemoteDMATransfer(dst_ids=[dst(d) for d, _ in places], dma_engine_mask=sum(1 << e for e in engines),
+                                                      remote_sem=T.sem[args], srcs=[ap(a) for a in srcs],
+                                                      dsts=[ap(p) for _, p in places], alu_op=len(srcs) - 1)
+                                    for engines, srcs, places in kw], local_sem=T.sem.sent)
+            elif name == "dma_start":
+                eng[q].dma_start(ap(args[0]), ap(args[1])).then_inc(T.sem[x["sem"][0]], 16)
+            else:
+                count[q] += 1
+                call[name](*[ap(a) for a in args], **{k: ap(v) for k, v in kw.items()}).then_inc(T.sem["q" + q], 1)
+        mark[i] = (x["sem"][0], x["sem"][1] or 0) if x["sem"] else ("q" + q, count[q])
+    for q in count:
+        totals["q" + q] = count[q]
     for sem in sorted(totals, key=lambda x: x[0] == "d"):
         if all(known[q].get(sem, 0) < totals[sem] for q in eng):
             wait("G", sem, totals[sem])

from concourse.bass import DstId, RemoteDMATransfer
from concourse.mybir import AluOpType as OP, AxisListType, ActivationFunctionType as AF

N, V, C, L, R = 8, 2048, 6144, 256, 3
W = V + L
BIAS = 32768.0
Q = C // 16
HALVES = "SSSSSVSSSVSSVSSS"
BULK = ("VSVSVSV", "VSVSVSV", "VSVSVSVS")

SCRATCH = {}
WIDTH = {"bfloat16": 2, "float16": 2, "uint16": 2, "float32": 4, "int32": 4}


def _sb(name, cols, dtype):
    SCRATCH[name] = ("sbuf", [128, cols], dtype)


for _n, _c, _d in [
    ("K", C, "bfloat16"), ("X", V, "bfloat16"), ("CD", V, "int32"), ("PA", 128, "int32"), ("META", C, "bfloat16"),
    ("BC", 2 * Q, "int32"), ("CP", 6 * Q, "bfloat16"), ("CI", Q, "bfloat16"), ("XB", 16 * L, "bfloat16"),
    ("XI", R * L, "bfloat16"), ("XO", 16 * R, "uint16"), ("i7", 16 * R, "float32"),
    ("W1", W, "bfloat16"), ("KW", W, "bfloat16"), ("UB", 2 * L, "bfloat16"), ("UL", 2 * L, "bfloat16"), ("KG", 4096, "bfloat16"), ("BA", 2048, "float16"),
    ("PC", V, "float16"), ("PX", 3 * L, "float16"), ("XS", L, "bfloat16"), ("XG", L, "bfloat16"), ("XL", 2 * L, "bfloat16"),
    ("KC", 272, "bfloat16"), ("KA", V, "bfloat16"),
    ("MS", 1568, "bfloat16"), ("MG", 512, "bfloat16"), ("E", L, "uint16"),
    ("i1", 144, "float32"), ("i3", 256, "float32"), ("i4", 128, "float32"), ("i5", 256, "float32"), ("i6", 256, "float32"),
    ("ii", 32, "int32"), ("col", 32, "float32"), ("I16", 16, "float32"), ("G8", 8, "float32"),
    ("ZA", 144, "float16"), ("ZT", 144, "bfloat16"), ("ZW", 144, "bfloat16"), ("ZC", 144, "bfloat16"), ("ZY", 144, "bfloat16"),
    ("ZR", 256, "bfloat16"), ("SZ", 288, "bfloat16"), ("SP", 288, "bfloat16"),
    ("ID", 128, "bfloat16"), ("BK", 128, "float16"), ("JJ", L, "float16"),
    ("IZ", 272, "bfloat16"), ("ZV", R * L, "bfloat16"), ("SW", 1040, "bfloat16"), ("ZK", 48, "bfloat16"),
    ("KP", 32, "bfloat16"), ("A2", 64, "bfloat16"),
    ("PF", 128, "float32"), ("S16", 16, "float16"), ("UX", L, "float16"), ("G", L, "float32"),
    ("EK", 2 * L, "float32"), ("UU", 144, "uint16"), ("U2", 32, "uint16"),
    ("f", 5120, "float32"), ("n", 512, "int32"), ("u", 512, "uint16"),
    ("OW", 24, "float32"), ("MK", L, "bfloat16"), ("OG", L, "float16"), ("YC", 48, "float32"),
    ("YP", 128, "float32"), ("P0", 128, "uint16"),
]:
    _sb(_n, _c, _d)
for _t in range(R):
    for _n, _c, _d in [("H", 16, "uint16"), ("sI", 896, "uint16"), ("lI", 448, "uint16"), ("sB", 4, "int32"), ("lB", 16, "int32"),
                       ("sX", 48, "uint16"), ("lU", 112, "uint16"), ("lL", 224, "uint16"),
                       ("sC", 128, "uint16"), ("lC", 112, "uint16"), ("sF", 8, "uint16"), ("lF", 16, "uint16")]:
        _sb("%s%d" % (_n, _t), _c, _d)
    _sb("P%d" % (_t + 1), 128, "uint16")
for _b in range(8):
    SCRATCH["ps%d" % _b] = ("psum", [128, 512], "float32")

SEMAPHORES = (["qV", "qS", "qP", "qG", "sent"] + ["d%d" % i for i in range(24)]
              + ["%s%d" % (x, t) for x in ("aF", "aS", "aB", "aU", "aL", "aC", "aD", "aI0", "aI1", "aI2", "aI3") for t in range(R)])

CYCLE, PE, GATHER, SCATTER, SIGNAL, START, ROW, BYTE, ISSUE = 0.83e-3, 0.42e-3, 1.56, 3.8, 0.05, 0.8, 0.012, 1 / 25e3, 0.3
PLAN = {}


def A(name, lo=0, hi=None, step=1, rows=(0, 128)):
    if hi is None:
        hi = SCRATCH[name][1][1]
    return ((name, (slice(*rows), slice(lo, hi, step))), [(name, lo, hi)], -(-(hi - lo) // step))


def I(win, off):
    return ((win[0], off[0], "indirect"), win[1] + off[1], 16 * off[2])


def hbm(name, *index):
    return ((name, index or (slice(None),)), [], 0)


def sl16(name, d, n=1):
    return A(name, 16 * d, 16 * (d + n))


def describe(r, cores, topo, steps, arrivals):
    hist, used, totals = {}, {"f": 0, "n": 0, "u": 0, "d": 0}, {"sent": 0}

    def step(q, calls, time, reads, writes, sem=None, rows=None, after=()):
        me = len(steps)
        hard, soft, banks = set(after), set(), set()
        for (name, lo, hi), wr in [(k, False) for k in reads] + [(k, True) for k in writes]:
            seen = hist.setdefault(name, [])
            if name.startswith("ps"):
                banks.add(name)
            for l2, h2, w2, q2, i in seen:
                if q == q2 == "P":
                    if name in banks:
                        soft.add(i)
                elif l2 < hi and lo < h2 and (wr or w2):
                    hard.add(i)
            if wr:
                seen[:] = [x for x in seen if not (lo <= x[0] and x[1] <= hi) or x[4] == me]
            seen.append((lo, hi, wr, q, me))
        hard.discard(me)
        soft.discard(me)
        steps.append({"rank": r, "q": q, "calls": calls, "time": time, "hard": hard, "soft": soft, "banks": banks, "sem": sem,
                      "rows": rows})
        return me

    def new(pool, cols=16):
        used[pool] += -(-cols // 8) * 8
        return A(pool, used[pool] - -(-cols // 8) * 8, used[pool] - -(-cols // 8) * 8 + cols)

    def cut(a, lo, hi, by=1):
        name, base, _ = a[1][0]
        return A(name, base + lo, base + hi, by)

    def laced(name, lo, b):
        return (A(name, lo + b, lo + 2 * L, 2)[0], [(name, lo + L * b, lo + L * b + L)], L)

    def both(name, base, lo, hi, by=1):
        a = A(name, base + lo, base + hi, by)
        return (a[0], [(name, base, base + 2 * L)], a[2])

    def keys(ins):
        return [k for a in ins if isinstance(a, tuple) for k in a[1]]

    def op(q, name, args, cycles, kw=None):
        out, ins = args[0], list(args[1:]) + list((kw or {}).values())
        if len(out[0]) == 3:
            time = 0.05 + out[2] * SCATTER * CYCLE
        elif isinstance(args[1], tuple) and len(args[1][0]) == 3:
            time = 0.06 + out[2] * GATHER * CYCLE
        else:
            time = (0.03 if q == "V" else 0.06) + max(64, cycles) * CYCLE
        step(q, [(name, args, kw or {})], time, keys(ins) + out[1][1:], out[1][:1])

    def short(*ops):
        return 0.5 if all(WIDTH[SCRATCH[a[1][0][0]][2]] == 2 for a in ops) else 1

    def copy(out, a):
        op("V", "tensor_copy", (out, a), out[2] * short(out, a))

    def tt(out, a, b, o):
        op("V", "tensor_tensor", (out, a, b, o), out[2] * (1 if "ps" in (a[1][0][0][:2], b[1][0][0][:2]) else 2))

    def ts(out, a, s1, o0, s2=None, o1=None):
        op("V", "tensor_scalar", (out, a, s1, s2, o0) + ((o1,) if o1 else ()), out[2] * short(out, a))

    def red(out, a, o, absolute=False):
        op("V", "tensor_reduce", (out, a, AxisListType.X, o), a[2], {"apply_absolute_value": absolute})

    def fill(out, v):
        op("V", "memset", (out, v), out[2] * short(out))

    def act(out, a, fn=AF.Copy, **kw):
        op("S", "activation", (out, a, fn), out[2], kw)

    def mms(group):
        step("P", [("matmul", m, {}) for m in group], sum(0.013 + max(min(64, m[1][2]), m[2][2]) * PE for m in group),
             [k for m in group for k in m[1][1] + m[2][1]], [k for m in group for k in m[0][1]])

    def iota(out, pattern, base, mult):
        kw = {} if SCRATCH[out[1][0][0]][2] == "int32" else {"allow_small_or_imprecise_dtypes": True}
        step("G", [("iota", (out, pattern, base, mult), kw)], 0.13 + 2 * out[2] * CYCLE, [], out[1])

    def dmas(q, pairs, rows, size, sem=None, reads=(), after=()):
        if sem is None:
            used["d"] += 1
            sem = ("d%d" % (used["d"] - 1), 16 * len(pairs))
            totals[sem[0]] = sem[1]
        return step(q, [("dma_start", p, {}) for p in pairs], 0.05 * len(pairs), keys([p[1] for p in pairs]) + list(reads),
                    keys([p[0] for p in pairs]), sem, (rows, size), after)

    def conv(out, z, src, start=True, stop=True):
        mms([(out, A(z, 15 - i, 143 - i), src(i), start and i == 0, stop and i == 15) for i in range(16)])

    core = cores[r]
    peers = [(r + i) % N for i in range(1, N)]
    lanes = topo.engines(core, cores[peers[0]])

    def slot(d):
        return (d - r - 1) % N

    def send(sem, transfers):
        src = transfers[0][1][0]
        size = src[2] * WIDTH[SCRATCH[src[1][0][0]][2]]
        rows = max(128 * len(x[2]) * len(lanes) // len(x[0]) for x in transfers)
        me = step("G", [("remote", sem, transfers)], ISSUE, keys([a for x in transfers for a in x[1]]), [], ("sent", 0), (rows, size))
        for engines, _, places in transfers:
            totals["sent"] += len(engines)
            for d, _ in places:
                arrivals.setdefault((d, sem), []).append((me, len(engines)))

    def landed(sem, where, own=None):
        me = step("", [], 0.0, [], where[1] if isinstance(where, tuple) else where, (sem, None))
        if own is not None:
            arrivals.setdefault((r, sem), []).append((own, 16))
        arrivals[(r, sem, "step")] = me

    def deal(sem, dests, src, land):
        far = [d for d in dests if topo.die(cores[d]) != topo.die(core)]
        near = [d for d in dests if d not in far]
        w = len(lanes) >> (len(dests) - 1).bit_length()
        pool = lanes[0::2] + lanes[:0:-2]
        send(sem, [(side[w * i:w * i + w], src(d), [(d, land(d))]) for group, side in ((far, pool), (near, pool[::-1]))
                   for i, d in enumerate(group)])

    def share(sem, src, land, dests=peers):
        send(sem, [(lanes, [src], [(d, land(d)) for d in dests])])

    def share_list(sem, src, name):
        place = A(name, 2 * r, 2 * r + 2)
        share(sem, src, lambda d: place)
        landed(sem, A(name), dmas("Y", [((place[0], [], 2), src)], 128, 8, (sem, None)))

    def tree(own, land, w):
        cv, tr, out = new("f", 8 * w), new("f", 6 * w), new("f", w)
        own(cut(cv, 7 * w, 8 * w))
        copy(cut(cv, 0, 7 * w), A(land))
        tt(cut(tr, 0, 4 * w), cut(cv, 0, 4 * w), cut(cv, 4 * w, 8 * w), OP.add)
        tt(cut(tr, 4 * w, 6 * w), cut(tr, 0, 2 * w), cut(tr, 2 * w, 4 * w), OP.add)
        tt(out, cut(tr, 4 * w, 5 * w), cut(tr, 5 * w, 6 * w), OP.add)
        return out

    last = []
    for name, src, size in (("PA", "pa", 512), ("CD", "cd", 4 * V), ("X", "xv", 2 * V), ("K", "kc", 2 * C)):
        last = [dmas("Y", [(A(name), hbm(src))], 128, size, after=last and [])]
    dmas("S", [(A("BC", 0, Q), hbm("bt"))], 128, 4 * Q)
    dmas("S", [(A("BC", Q, 2 * Q), hbm("co"))], 128, 4 * Q)

    cA, cG, cQ, c8, cJ, cH, c15, cT, cW, cC, cV, cS, cS2, cY, cP, cG2 = [A("col", i, i + 1) for i in range(16)]
    half, bias, minus, pays = [A("col", 16 + 2 * i, 18 + 2 * i) for i in range(4)]
    row6, row7, row8 = A("I16", 6, 7), A("I16", 7, 8), A("I16", 8, 9)
    LN, SPARE, VN, VA, ZS, VO, CB = new("f", 2), new("f", 2), new("f"), new("f"), new("f"), new("f"), new("f")
    iota(A("ii", 0, 1), [[0, 1]], 0, 1)
    iota(A("i3"), [[0, 16], [1, 16]], 0, 0)
    iota(A("i4"), [[1, 8], [0, 16]], 0, 0)
    iota(A("i5"), [[1, 256]], 0, 0)
    iota(A("i1"), [[1, 144]], 0, -1)
    iota(A("CI"), [[1, Q]], -Q // 2, 0)
    iota(A("i6"), [[100, 8], [0, 2], [1, 16]], -400, 0)
    iota(A("i7"), [[L, R], [16, 2], [32, N]], 0, 0)
    iota(A("KP"), [[16384, 16], [0, 2]], 0, 0)
    for name in ("IZ", "KC", "MS", "OW"):
        iota(A(name, 0, 16), [[0, 16]], 0, 0)
    iota(A("MS", 528, 800), [[0, 272]], 0, 0)
    for i in range(2):
        fill(A("XB", 4 * L * i, 4 * L * i + 4 * L), 0.0)
    for i in range(3):
        iota(A("W1", W // 3 * i, W // 3 * i + W // 3), [[0, W // 3]], 0, 0)
        fill(A("KW", W // 3 * i, W // 3 * i + W // 3), 0.0)
    fill(A("SW", 2, 1040), 0.0)
    for i, (shift, mask) in enumerate(((0, 15), (4, 7), (5, 3), (1, 7), (0, 1), (4, 1))):
        ts(A("ii", 1 + i, 2 + i), A("ii", 0, 1), shift, OP.arith_shift_right, mask, OP.bitwise_and)
    copy(A("col", 0, 6), A("ii", 1, 7))
    ts(A("I16"), A("i3", 0, 16), cA, OP.is_equal)
    for i in range(2):
        ts(A("SW", i, i + 1), A("I16", 0, 1), 2.0 * i - 1.0, OP.mult)
    ts(A("XO"), A("i7"), cA, OP.add)
    ts(half, A("i5", 0, 2), cJ, OP.is_equal)
    ts(bias, half, BIAS, OP.mult)
    ts(minus, half, -1.0, OP.mult)
    ts(A("BK"), A("i4"), cG, OP.is_equal)
    ts(A("JJ"), A("i5"), A("I16", 0, 1), OP.mult, 1.0 / 512, OP.mult)
    for a in range(16):
        ts(A("BA", 128 * a, 128 * a + 128), A("BK"), A("I16", a, a + 1), OP.mult)
    ts(c15, cA, -1.0, OP.mult, 15.0, OP.add)
    ts(VN, A("i5", 0, 256, 16), cA, OP.add)
    ts(LN, cut(VN, 2 * r, 2 * r + 2), 1.0 / 512, OP.mult)
    ts(SPARE, cut(VN, 2 * r, 2 * r + 2), float(V), OP.add)
    ts(A("G8"), A("i5", 0, 8), cG, OP.is_equal)
    red(cT, A("I16", 0, 3), OP.add)
    red(cW, A("I16", 3, 6), OP.add)
    tt(cC, row8, row6, OP.add)
    tt(cY, row6, row7, OP.add)
    ts(cV, cW, 2.0 ** -23, OP.mult)
    ts(cS, c8, 16.0, OP.mult, 3.0, OP.add)
    ts(cS2, cQ, 4.0, OP.mult, cS, OP.add)
    ts(cP, cH, -8192.0, OP.mult, 8192.0, OP.add)
    ts(pays, half, cP, OP.mult)
    ts(cG2, cG, 2.0, OP.mult)
    ts(A("ZA"), A("i1"), c15, OP.is_equal)
    ts(A("ID"), A("i1", 0, 128), 0.0, OP.is_equal)
    for name, weight in (("ZY", cY), ("ZW", cV), ("ZC", cC), ("ZT", cT)):
        ts(A(name), A("i1"), c15, OP.is_equal, weight, OP.mult)
    ts(A("ZR"), A("i6"), cG2, OP.is_equal, cT, OP.mult)
    for b in range(2):
        ts(A("SZ", 144 * b, 144 * b + 144), A("i5", 0, 144), cS2, OP.is_equal, cut(half, b, b + 1), OP.mult)
        ts(A("SP", 144 * b, 144 * b + 144), A("i5", 0, 144), cS2, OP.is_equal, cut(pays, b, b + 1), OP.mult)
    fill(A("ZK", 0, 2), 0.5)
    fill(A("ZK", 2, 34), -1.0)
    ts(A("ZV", 0, L), A("i5"), 1.0, OP.add, row7, OP.mult)
    for i in range(1, R):
        z = new("f", 1)
        act(z, row6, AF.Identity, scale=float(L * i))
        act(A("ZV", L * i, L * i + L), A("ZV", 0, L), AF.Identity, bias=z)
    act(A("EK", 0, L), A("i3"), AF.Abs, bias=cA, scale=-1.0)
    act(A("IZ", 16, 272), A("EK", 0, L), AF.Relu, bias=1.0, scale=-1.0)
    if r < R:
        act(ZS, VN, AF.Identity, bias=1.0)
        act(VO, VN, AF.Identity, bias=float(L * r + 4096))
    copy(A("P0"), A("PA"))
    for b in range(2):
        copy(A("H0", 8 * b, 8 * b + 8), A("PA", b, 16, 2))

    ts(VA, A("i3", 0, 16), float(Q), OP.mult, Q / 2, OP.add)
    ts(CB, VA, row8, OP.mult)
    for i in range(16):
        act(A("META", Q * i, Q * i + Q), A("CI"), AF.Identity, bias=cut(CB, i, i + 1), scale=row6)
    for i in range(2):
        rest = A("ps%d" % (1 + i), 0, Q)
        copy(A("CP", i * Q, i * Q + Q), A("BC", i * Q, i * Q + Q))
        tt(rest, A("BC", i * Q, i * Q + Q), A("CP", i * Q, i * Q + Q), OP.subtract)
        act(A("CP", (2 + i) * Q, (3 + i) * Q), rest)
        tt(A("CP", (4 + i) * Q, (5 + i) * Q), rest, A("CP", (2 + i) * Q, (3 + i) * Q), OP.subtract)
    dmas("Y", [((("META", (slice(row, 128, 16), slice(None))), A("META")[1], 0), A("CP", part * Q, part * Q + Q))
               for row, part in enumerate((0, 2, 4, 1, 3, 5))], 6 * 128, 2 * Q, reads=A("K")[1])

    for t in range(R):
        P, Pn = "P%d" % t, "P%d" % (t + 1)
        lead = t + 1 if t + 1 < R else None
        s = sl16(P, t)
        sI, lI, lB, lF, sX = "sI%d" % t, "lI%d" % t, A("lB%d" % t), A("lF%d" % t), "sX%d" % t

        def slot_list(out, src):
            ts(out, src, float(L * t), OP.max, float(15 - L * t), OP.add)

        act(A("XI", L * t, L * t + L), I(A("X"), sl16("XO", t)))
        dmas("Y", [(A("XB", b * L, b * L + L, rows=(16 * b, 16 * b + 16)), A("XI", L * t, L * t + L, rows=(16 * b, 16 * b + 16)))
                   for b in range(8)], 128, 2 * L)
        copy(A("E"), I(A("CD"), A("H%d" % t)))
        act(A("XS"), I(A("X"), A("H%d" % t)))
        for b in range(8):
            ts(A("XB", (8 + b) * L, (9 + b) * L), A("XS"), A("G8", b, b + 1), OP.mult)
        if t:
            for b in range(2):
                copy(A(P, 16 * t + b, 16 * t + 16, 2), A("H%d" % t, 8 * b, 8 * b + 8))

        sf, neg, off, inside, low, aim, gap, no = [new("f", 2) for _ in range(8)]
        copy(A("S16"), s)
        copy(sf, cut(s, 2 * r, 2 * r + 2))
        mms([(A("ps4", 0, 256), A("BK"), A("JJ"), True, False)]
            + [(A("ps4", a, 256, 16), A("BA", 128 * a, 128 * a + 128), A("S16"), False, a == 15) for a in range(16)])
        act(neg, sf, AF.Identity, scale=-1.0)
        act(off, sf, AF.Abs, bias=-(L * t + 127.5))
        act(inside, off, AF.Relu, bias=128.0, scale=-1.0)
        tt(aim, inside, LN, OP.add)
        tt(gap, SPARE, sf, OP.subtract)
        for b in range(2):
            act(A("EK", L * b, L * b + L), A("ps4", 0, 256), AF.Abs, bias=cut(neg, b, b + 1))
            red(cut(low, b, b + 1), A("EK", L * b, L * b + L), OP.min)
            ts(cut(no, b, b + 1), cut(low, b, b + 1), cut(aim, b, b + 1), OP.not_equal, cut(gap, b, b + 1), OP.mult)
            ts(A("sF%d" % t, b, b + 1), cut(no, b, b + 1), cut(sf, b, b + 1), OP.add)
        share_list("aF%d" % t, A("sF%d" % t, 0, 2), "lF%d" % t)

        for i, d in enumerate(peers + [r]):
            bank, c0 = ("ps%d" % (i // 2 % 2), 128 * (i % 2)) if d != r else ("ps2", 0)
            for b in range(2):
                (copy if HALVES[2 * i + b] == "V" else act)(laced("KG", 2 * L * d, b), I(A("K"), sl16("E", 8 * b + d)))
            for h in range(2):
                mms([(A(bank, c0 + 32 * (a % 4), c0 + 32 * (a % 4) + 32, rows=(32 * (a // 4), 32 * (a // 4) + 32)),
                      A("XB", 16 * d + a, 16 * L, 128), both("KG", 2 * L * d, 32 * a, 32 * a + 32), True, True)
                     for a in range(8 * h, 8 * h + 8)])
            if d != r and (i % 2 or i == N - 2):
                j = i // 2
                lo, hi = 128 * j, 64 * i + 64
                for b in range(2):
                    ts(A(sI, 448 * b + lo, 448 * b + hi), A(bank, b, c0 + 128, 2), cut(half, b, b + 1), OP.mult,
                       cut(bias, b, b + 1), OP.add)
                deal("aI%d%d" % (j, t), peers[2 * j:2 * j + 2],
                     lambda d: [A(sI, 448 * b + 64 * slot(d), 448 * b + 64 * slot(d) + 64) for b in range(2)],
                     lambda d: A(lI, 64 * slot(d), 64 * slot(d) + 64))
                landed("aI%d%d" % (j, t), A(lI, lo, hi))

        for b in range(2):
            act(laced("MG", 0, b), I(A("META"), sl16("E", 8 * b + r)))
        mms([(A("ps3", 0, 64), A("ZR", 128 - 32 * (o // 2) - o % 2, 256 - 32 * (o // 2) - o % 2),
              both("MG", 0, 128 * (o // 2) + o % 2, 128 * (o // 2) + 128, 2), o == 0, o == 7) for o in range(8)])
        z, pay = A("ps5", 2, 34), A("ps6", 0, 32)
        mms([(A("ps5", 0, 34), A("ID"), A("ZK", 0, 34), True, False)])
        conv(z, "ZW", lambda a: both("MG", 0, 32 * a, 32 * a + 32), False, False)
        mms([(pay, A("ID"), A("KP"), True, False)])
        conv(pay, "ZC", lambda a: both("MG", 0, 32 * a, 32 * a + 32), False, False)
        thr, a0_, a1_, a2_, y0, y1 = new("f", 64), new("f", 64), new("f", 64), new("f", 64), new("f", 128), new("f", 128)
        own = new("f", 128)
        for b in range(2):
            act(cut(own, 64 * b, 64 * b + 64), A("ps2", b, 128, 2), AF.Identity, scale=cut(minus, b, b + 1),
                bias=(1 - b) * (7 * BIAS + 0.5))
        tt(thr, cut(own, 0, 64), A("ps3", 0, 64), OP.add)
        tt(a0_, thr, cut(own, 64, 128), OP.add)
        copy(y0, A(lI, 0, 128))
        copy(A("ps2", 128, 256), A(lI, 128, 256))
        tt(y1, A("ps2", 128, 256), y0, OP.add)
        copy(A("ps2", 256, 384), A(lI, 256, 384))
        tt(A("ps2", 128, 256), A("ps2", 256, 384), y1, OP.add)
        tt(a1_, a0_, A("ps2", 128, 192), OP.subtract)
        tt(a2_, a1_, A("ps2", 192, 256), OP.subtract)

        copy(A("ps2", 448, 512), A(lI, 384, 448))
        tt(A("A2"), A("ps2", 448, 512), a2_, OP.is_gt)
        for name, out in (("SZ", z), ("SP", pay)):
            mms([(cut(out, b, 32, 2), A(name, 144 * b + 3 - h, 144 * b + 131 - h), sl16("A2", h), False, b == 1 and h == 3)
                 for b in range(2) for h in range(4)])
        least, over, key = new("f", 2), new("f", 32), new("f", 32)
        for b in range(2):
            red(cut(least, b, b + 1), A("ps5", b, 34, 2), OP.min, True)
            ts(cut(over, b, 32, 2), cut(z, b, 32, 2), cut(least, b, b + 1), OP.not_equal, 2.0 ** 23, OP.mult)
        tt(key, over, pay, OP.add)
        for b in range(2):
            red(A("sB%d" % t, b, b + 1), cut(key, b, 32, 2), OP.min)
        share_list("aB%d" % t, A("sB%d" % t, 0, 2), "lB%d" % t)

        cand, okN, e3 = new("f", 32), new("f"), new("f")
        copy(I(A("W1"), lF), A("ZV", L * t, L * t + L))
        ts(okN, lF, float(V), OP.is_lt)
        if lead is not None:
            act(A("UL", 0, L), I(A("W1"), sl16(P, lead)))
            act(A("UL", L, 2 * L), A("W1", L * lead, L * lead + L))
            conv(A("ps7", 288, 320), "ZY", lambda a: A("UL", a, 2 * L, 16))
            slot_list(A("U2"), A("ps7", 288, 320))
            if r == lead:
                act(cut(cand, 0, 16), A("ps7", 288, 304), AF.Identity, bias=4095.0)
                act(cut(cand, 16, 32), A("ps7", 304, 320), AF.Identity, bias=8191.0)
            dmas("Y", [(A("XL", 0, L), hbm("xv", slice(None), slice(L * lead, L * lead + L)))], 128, 2 * L)
            act(A("XL", L, 2 * L), I(A("X"), sl16(P, lead)))
        order_c = [d for d in peers + [r] if d != lead]
        nc = len(order_c)
        chunks = [(0, nc)] if lead is not None else [(0, 4), (4, 7), (7, 8)]
        below = r != t
        if r != lead:
            act(A("UB", 0, L), I(A("W1"), sl16(P, r)))
            if below:
                act(A("UB", L, 2 * L), A("W1", L * r, L * r + L))
            conv(sl16("ps7", 0, 1 + below), "ZY", lambda a: A("UB", a, L + L * below, 16))
            slot_list(sl16("UU", 0, 1 + below), sl16("ps7", 0, 1 + below))
            act(cut(cand, 0, 16), sl16("ps7", 0), AF.Identity, bias=4095.0)

        n0, n1, n2, sh, sl, upu = new("n"), new("n"), new("n"), new("u"), new("u"), new("u")
        copy(n0, s)
        copy(A("PF"), A(P))
        ts(n1, n0, 4, OP.arith_shift_right)
        ts(n2, n0, 15, OP.bitwise_and)
        copy(sh, n1)
        copy(sl, n2)
        act(A("G"), I(A("PF"), sh))
        tt(A("UX"), I(A("I16"), sl), A("G"), OP.mult)
        conv(A("ps4", 320, 336), "ZA", lambda a: A("UX", a, L, 16))
        copy(upu, A("ps4", 320, 336))
        act(A("XG"), I(A("X"), upu))

        if r != lead:
            n3, n4, ao, e2 = new("n"), new("n"), new("u"), new("f")
            if r == t:
                act(e3, A("ps4", 320, 336), AF.Identity, bias=8192.0)
                tt(e2, ZS, okN, OP.mult)
                ts(sl16("UU", 1), e2, 15.0, OP.add)
                ts(n3, e2, 15.0, OP.add)
                tt(e2, cut(cand, 0, 16), VO, OP.not_equal)
                tt(cut(cand, 0, 16), cut(cand, 0, 16), e2, OP.mult)
            else:
                slot_list(n3, sl16("ps7", 1))
                act(e3, sl16("ps7", 1), AF.Identity, bias=8191.0)
            ts(n4, n3, 4, OP.arith_shift_right)
            copy(ao, n4)
            act(A("MK"), I(A("IZ"), sl16("UU", 1)))

        m0, m1, cu, fo = new("n"), new("n"), new("u"), new("u")
        ts(m0, lB, 8191, OP.bitwise_and)
        copy(cu, m0)
        act(A("KC", 16, 272), I(A("K"), cu))
        tt(A("PX", 0, L), I(A("K"), cu), A("XG"), OP.mult)
        nx = 48 if lead is not None else 16
        if lead is not None:
            tt(A("PX", L, 3 * L), I(A("KC"), A("U2")), A("XL"), OP.mult)
        conv(A("ps6", 64, 64 + nx), "ZA", lambda a: A("PX", a, 16 * nx, 16))
        ts(A(sX, 0, nx), A("ps6", 64, 64 + nx), BIAS, OP.add)
        if lead is not None and r != lead:
            share("aL%d" % t, A(sX, 16, 48), lambda d: A("lL%d" % t, 32 * slot(d), 32 * slot(d) + 32), [lead])
        share("aU%d" % t, A(sX, 0, 16), lambda d: sl16("lU%d" % t, slot(d)), [d for d in peers if d != lead])

        nm = 48 if r == lead else 32
        mine_u = A("U2") if r == lead else sl16("UU", 0)
        sign = A("ps3", 113, 161)
        hT, c1, c2, c3, a1 = new("f", 48), new("f"), new("f"), new("f"), new("f")
        ts(m1, lB, 13, OP.arith_shift_right, 1025, OP.bitwise_and)
        copy(fo, m1)
        act(A("MS", 16, 272), I(A("META"), cu))
        act(A("MS", 272, 16 + 16 * nm), I(A("MS", 0, 272), mine_u))
        act(A("MS", 800, 1056), I(A("SW"), fo))
        act(A("MS", 1056, 800 + 16 * nm), I(A("MS", 784, 1056), mine_u))
        conv(A("ps3", 64, 113 + nm), "ZT", lambda a: A("MS", 16 + a, 800 + 16 * nm, 16))
        act(cut(hT, 0, nm), A("ps3", 64, 64 + nm), AF.Identity, bias=7 * BIAS + 0.5)
        conv(A("ps4", 256, 272), "ZW", lambda a: A("MS", 16 + a, 272, 16))
        act(c1, A("ps4", 256, 272), AF.Identity, bias=1.0, scale=2.0 ** 23)
        act(a1, cut(sign, 0, 16), AF.Abs)
        tt(c2, c1, okN, OP.mult)
        tt(c3, c2, a1, OP.mult)
        act(sl16("YC", t), c3, AF.Identity, bias=-1.0)

        copy(I(A("KW"), lF), A("KC", 16, 272))
        by_s = [d for i, d in enumerate(order_c) if BULK[t][i] == "S"]
        for i, d in enumerate(by_s):
            mms([(A("ps%d" % (i % 2), L * (i // 2), L * (i // 2) + L), A("ID"), A("X", L * d, L * d + L), True, True)])
        for j, (lo, hi) in enumerate(chunks):
            bank = ("ps7", "ps2", "ps7")[j]
            for i in range(lo, hi):
                d = order_c[i]
                if d in by_s:
                    k = by_s.index(d)
                    act(A("KA", L * i, L * i + L), I(A("KW"), sl16(P, d)))
                    tt(A("PC", L * i, L * i + L), A("KA", L * i, L * i + L), A("ps%d" % (k % 2), L * (k // 2), L * (k // 2) + L), OP.mult)
                else:
                    tt(A("PC", L * i, L * i + L), I(A("KW"), sl16(P, d)), A("X", L * d, L * d + L), OP.mult)
            conv(A(bank, 144 + 16 * lo, 144 + 16 * hi), "ZA", lambda a: A("PC", L * lo + a, L * hi, 16))
            dests = [d for d in order_c[lo:hi] if d != r]
            if dests:
                ts(sl16("sC%d" % t, lo, len(dests)), sl16(bank, 9 + lo, len(dests)), BIAS, OP.add)
                deal("aC%d" % t, dests, lambda d: [sl16("sC%d" % t, order_c.index(d))], lambda d: sl16("lC%d" % t, slot(d)))

        best, low11, N0, N1 = new("n"), new("n"), new("f"), new("f")
        Po, mine = sl16("PF", r), sl16(Pn, r)

        def moves(d, sign):
            x, y = new("f", d[2]), new("f", d[2])
            tt(x, d, sign, OP.mult)
            ts(y, x, 0.0, OP.is_gt)
            return x, y

        if r == lead:
            landed("aL%d" % t, A("lL%d" % t))
            x, y = moves(tree(lambda o: tt(o, A("ps6", 80, 112), cut(hT, 16, 48), OP.subtract), "lL%d" % t, 32), cut(sign, 16, 48))
            tt(x, y, cand, OP.mult)
            tt(N0, cut(x, 0, 16), cut(x, 16, 32), OP.max)
            tt(best, N0, Po, OP.max)
        else:
            landed("aU%d" % t, A("lU%d" % t))
            dU, x = tree(lambda o: tt(o, A("ps6", 64, 80), cut(hT, 0, 16), OP.subtract), "lU%d" % t, 16), new("f")
            tt(x, dU, cut(sign, 0, 16), OP.mult)
            ts(A("OW", 1, 17), x, 0.0, OP.is_gt)
            tt(A("OG"), I(A("OW", 0, 17), ao), A("MK"), OP.mult)
            conv(A("ps5", 128, 144), "ZA", lambda a: A("OG", a, L, 16))
            tt(N0, e3, A("ps5", 128, 144), OP.mult)
            tt(N1, N0, Po, OP.max)
            landed("aC%d" % t, A("lC%d" % t))
            x, y = moves(tree(lambda o: tt(o, sl16("ps7", 8 + nc), cut(hT, 16, 32), OP.subtract), "lC%d" % t, 16), cut(sign, 16, 32))
            tt(x, y, cut(cand, 0, 16), OP.mult)
            tt(best, x, N1, OP.max)
        ts(low11, best, 2047, OP.bitwise_and)
        if r == lead:
            mine = A("H%d" % lead)
            for b in range(2):
                copy(cut(mine, 8 * b, 8 * b + 8), cut(low11, b, 16, 2))
        else:
            copy(mine, low11)
        share("aS%d" % t if r == lead else "aD%d" % t, mine, lambda d: mine)
        if lead is not None and r != lead:
            landed("aS%d" % t, A("H%d" % lead))
        landed("aD%d" % t, [sl16(Pn, d)[1][0] for d in peers if d != lead])

    dmas("S", [(hbm("yc"), A("YC"))], 128, 192)
    copy(A("YP"), A("P%d" % R))
    dmas("Y", [(hbm("yp"), A("YP"))], 128, 512)
    return totals


def arrange(steps):
    n = len(steps)
    follow = [[] for _ in range(n)]
    for i, x in enumerate(steps):
        for j in x["hard"] | x["soft"]:
            follow[j].append(i)
    flight = [START + x["rows"][0] / 16 * (ROW + x["rows"][1] * BYTE) if x["rows"] else 0.0 for x in steps]
    left = [len(x["hard"] | x["soft"]) for x in steps]
    topo_order, todo, count = [], [i for i in range(n) if not left[i]], list(left)
    while todo:
        i = todo.pop()
        topo_order.append(i)
        for j in follow[i]:
            count[j] -= 1
            if not count[j]:
                todo.append(j)
    way = [0.0] * n
    for i in reversed(topo_order):
        way[i] = steps[i]["time"] + flight[i] + SIGNAL + max([way[j] for j in follow[i]] or [0.0])
    free, engines, bank, begin, end, ready = {}, {}, {}, [0.0] * n, [0.0] * n, {}

    def release(i):
        x = steps[i]
        if x["q"]:
            ready.setdefault((x["rank"], x["q"]), []).append(i)
        else:
            finish(i, max(end[j] for j in x["hard"]))

    def finish(i, at):
        end[i] = at
        for j in follow[i]:
            left[j] -= 1
            if not left[j]:
                release(j)

    def earliest(i):
        x = steps[i]
        times = [free.get((x["rank"], x["q"]), 0.0)] + [end[j] + SIGNAL for j in x["hard"]]
        for b in x["banks"]:
            times += [end[j] + SIGNAL for q, j in bank.get((x["rank"], b), {}).items() if q != x["q"]]
        return max(times)

    for i in [i for i in range(n) if not left[i]]:
        release(i)
    order = []
    while any(ready.values()):
        pick = None
        for key, waiting in ready.items():
            if waiting:
                at = {i: earliest(i) for i in waiting}
                first = min(waiting, key=lambda i: at[i] - way[i])
                fits = [i for i in waiting if at[i] + steps[i]["time"] <= at[first] + SIGNAL and i != first]
                if fits:
                    first = min(fits, key=lambda i: (at[i] - way[i]))
                if pick is None or at[first] < pick[0]:
                    pick = (at[first], first, key)
        at, i, key = pick
        x = steps[i]
        ready[key].remove(i)
        order.append(i)
        for b in x["banks"]:
            seen = bank.setdefault((x["rank"], b), {})
            x["hard"] = x["hard"] | {j for q, j in seen.items() if q != x["q"]}
            seen[x["q"]] = i
        free[key] = at + x["time"]
        done = free[key]
        if x["rows"]:
            done = max(done + START, engines.get(x["rank"], 0.0)) + flight[i] - START
            engines[x["rank"]] = done
        finish(i, done)
    return order


def rank_program(g, core, T, topo):
    r = T.rank_of(core)
    if r is None:
        return
    if not PLAN:
        steps, arrivals = [], {}
        totals = [describe(d, T.cores, topo, steps, arrivals) for d in range(N)]
        for key in [k for k in arrivals if len(k) == 2]:
            x = steps[arrivals[key + ("step",)]]
            x["hard"] = x["hard"] | {i for i, _ in arrivals[key]}
            x["sem"] = (key[1], sum(k for _, k in arrivals[key]))
            totals[key[0]][key[1]] = x["sem"][1]
        PLAN.update(steps=steps, order=arrange(steps), totals=totals)
    steps, totals = PLAN["steps"], dict(PLAN["totals"][r])
    eng = {"V": g.vector, "S": g.scalar, "P": g.tensor, "G": g, "Y": g.sync}
    call = {"tensor_copy": g.vector.tensor_copy, "tensor_tensor": g.vector.tensor_tensor, "tensor_scalar": g.vector.tensor_scalar,
            "tensor_reduce": g.vector.tensor_reduce, "memset": g.vector.memset, "activation": g.scalar.activation,
            "matmul": g.tensor.matmul, "iota": g.iota}
    known = {q: {} for q in eng}
    count = {q: 0 for q in "VSPG"}
    mark = {}

    def ap(a):
        if not isinstance(a, tuple):
            return a
        if len(a[0]) == 3:
            return T[a[0][0][0]][a[0][0][1]].indirect(T[a[0][1][0]][a[0][1][1]])
        return T[a[0][0]][a[0][1]]

    def wait(q, sem, val):
        if known[q].get(sem, 0) < val:
            eng[q].wait_ge(T.sem[sem], val)
            known[q][sem] = val

    def dst(d):
        rid, pid, _ = topo.addr(T.cores[d])
        return DstId(rid=rid, pnc=pid)

    def needs(i):
        out = []
        for j in steps[i]["hard"]:
            if steps[j]["q"]:
                out.append(mark[j])
            else:
                out.append(steps[j]["sem"])
        return out

    for i in PLAN["order"]:
        x = steps[i]
        if x["rank"] != r:
            continue
        q, need = x["q"], {}
        for sem, val in needs(i):
            need[sem] = max(need.get(sem, 0), val)
        for sem in need:
            wait(q, sem, need[sem])
        for name, args, kw in x["calls"]:
            if name == "remote":
                g.remote_dma_fused([RemoteDMATransfer(dst_ids=[dst(d) for d, _ in places], dma_engine_mask=sum(1 << e for e in engines),
                                                      remote_sem=T.sem[args], srcs=[ap(a) for a in srcs],
                                                      dsts=[ap(p) for _, p in places], alu_op=len(srcs) - 1)
                                    for engines, srcs, places in kw], local_sem=T.sem.sent)
            elif name == "dma_start":
                eng[q].dma_start(ap(args[0]), ap(args[1])).then_inc(T.sem[x["sem"][0]], 16)
            else:
                count[q] += 1
                call[name](*[ap(a) for a in args], **{k: ap(v) for k, v in kw.items()}).then_inc(T.sem["q" + q], 1)
        mark[i] = (x["sem"][0], x["sem"][1] or 0) if x["sem"] else ("q" + q, count[q])
    for q in count:
        totals["q" + q] = count[q]
    for sem in sorted(totals, key=lambda x: x[0] == "d"):
        if all(known[q].get(sem, 0) < totals[sem] for q in eng):
            wait("G", sem, totals[sem])
